import numpy as np
import ml_dtypes


def mxq(x, axis, fmt="e4m3"):
    dtype, down = {"e4m3": (ml_dtypes.float8_e4m3fn, 7), "e5m2": (ml_dtypes.float8_e5m2, 14)}[fmt]
    v = np.moveaxis(np.asarray(x, np.float32).astype(ml_dtypes.bfloat16).astype(np.float64), axis, -1)
    blocks = v.reshape(v.shape[:-1] + (-1, 32))
    amax = np.abs(blocks).max(-1, keepdims=True)
    byte = np.maximum(np.where(amax > 0, np.frexp(amax)[1] - 1 + 127, 0) - down, 1)
    scale = np.exp2(byte - 127.0)
    codes = (blocks / scale).astype(np.float32).astype(dtype).astype(np.float64)
    return np.moveaxis((codes * scale).reshape(v.shape), -1, axis)


WIDE = False


def mx_kscale(k):
    if not WIDE:
        return np.ones(k)
    levels = np.array([10, -10, 5, -5, 0])
    if k % 512:
        return np.exp2(np.random.permutation(np.resize(levels, k // 32))).repeat(32)
    a = np.empty((k // 512, 16))
    for p in range(k // 512):
        a[p, :8] = np.random.permutation(np.resize(levels, 8))
        for g in range(8):
            far = levels[np.abs(levels - a[p, g]) >= 10]
            a[p, g + 8] = far[np.random.randint(len(far))]
    return np.exp2(a.ravel()).repeat(32)


def f64(x):
    return np.asarray(x).astype(np.float64)


def striped(idx):
    return np.tile(idx.reshape(-1, 16).T, (8, 1)).astype(np.uint16)


def unstriped(offs):
    return offs[:16].T.reshape(-1).astype(np.int64)


def pack_weight(w):
    k, n = w.shape
    w = f64(np.asarray(w, np.float32).astype(ml_dtypes.bfloat16)).reshape(k // 32, 32, n)
    amax = np.abs(w).max(1)
    byte = np.clip(np.where(amax > 0, np.frexp(amax)[1] - 1 + 127 - 7, 1), 1, 254)
    scaled = (w * np.exp2(127.0 - byte)[:, None, :]).reshape(k, n).astype(np.float32)
    words = np.ascontiguousarray(scaled.reshape(k // 512, 128, 4, n).transpose(0, 1, 3, 2)).astype(ml_dtypes.float8_e4m3fn).view(np.uint8)
    return words, np.ascontiguousarray(byte.astype(np.uint8).reshape(k // 512, 16, n))


def unpack_weight(words, scales):
    g, p, n, _ = words.shape
    vals = np.ascontiguousarray(words).view(ml_dtypes.float8_e4m3fn).astype(np.float64) * np.repeat(np.exp2(scales.astype(np.float64) - 127.0), 8, axis=1)[..., None]
    return vals.transpose(0, 1, 3, 2).reshape(g * 512, n)


K, T, E, C, N = 1536, 512, 8, 128, 128


def by_expert(wq, xq):
    return np.concatenate([wq[e].T @ xq[:, e * C:(e + 1) * C] for e in range(E)], axis=1)


def setup_inputs():
    n = np.random.standard_normal
    s = mx_kscale(K)[:, None]
    first = np.random.permutation(np.repeat(np.arange(E), T // E))
    second = (first + 1 + np.random.permutation(np.repeat(np.arange(E - 1), -(-T // (E - 1)))[:T])) % E
    while np.bincount(second, minlength=E).max() != T // E:
        load = np.bincount(second, minlength=E); hi, lo = int(load.argmax()), int(load.argmin())
        t = np.flatnonzero((second == hi) & (first != lo))[0]; second[t] = lo
    slot_token = np.empty(E * C, np.int64); pos = np.empty((2, T), np.int64); fill = np.zeros(E, np.int64)
    place = np.stack([np.random.permutation(C) for _ in range(E)])
    for r, deal in enumerate((first, second)):
        for t in np.random.permutation(T):
            e = deal[t]; j = e * C + place[e, fill[e]]; fill[e] += 1; slot_token[j] = t; pos[r, t] = j
    g = np.random.uniform(0.2, 0.8, T)
    packed = [pack_weight(m) for m in n((E, K, N)) / np.sqrt(K) / s[None]]
    return {
        "xT": (n((K, T)) * s).astype(np.float32),
        "w_words": np.stack([m[0] for m in packed]),
        "w_scales": np.stack([m[1] for m in packed]),
        "b": (0.3 * n((N, E))).astype(np.float32),
        "gate": np.stack([np.tile(g, (N, 1)), np.tile(1.0 - g, (N, 1))]).astype(np.float32),
        "offs": striped(slot_token),
        "pos1": striped(pos[0]),
        "pos2": striped(pos[1]),
    }


def reference(xT, w_words, w_scales, b, gate, offs, pos1, pos2):
    idx = unstriped(offs)
    xq = mxq(f64(xT)[:, idx], 0, "e4m3")
    w = np.stack([unpack_weight(w_words[e], w_scales[e]) for e in range(E)])
    y = by_expert(w, xq)
    y = y + np.repeat(f64(b), C, axis=1)
    return f64(gate[0]) * y[:, unstriped(pos1)] + f64(gate[1]) * y[:, unstriped(pos2)]

@@ -1,0 +1,166 @@
+from contextlib import ExitStack
+
+import concourse.mybir as mybir
+
+F32 = mybir.dt.float32
+BF16 = mybir.dt.bfloat16
+I32 = mybir.dt.int32
+U32 = mybir.dt.uint32
+U16 = mybir.dt.uint16
+U8 = mybir.dt.uint8
+FP8X4 = mybir.dt.float8_e4m3fn_x4
+MULT = mybir.AluOpType.mult
+ADD = mybir.AluOpType.add
+IDENTITY = mybir.ActivationFunctionType.Identity
+
+P = 128
+K, T, E, C, N = 1536, 512, 8, 128, 128
+SLOTS = E * C
+PASSES = K // 512
+FLOPS = 2 * K * N * SLOTS
+WORD_COLUMNS = (1376, 1376, 512)
+SCALE_COLUMNS = 704
+HALVES = ((0, 256), (256, 512))
+VECTOR_TOKENS = ((128, 128), (0, 0), (0, 0))
+LOADS = (((0, 512),), HALVES, HALVES)
+SCALE_CUTS = (0, 512, 1024)
+LAST_CUTS = (0, 384, 768, 1024)
+
+
+def interleave(copy, grouped, raw, lo, hi):
+    copy(
+        out=grouped[:, lo:hi, :].rearrange("p (c i) j -> p c j i", i=4),
+        in_=raw[:, :, lo:hi].rearrange("p j (c i) -> p c j i", i=4),
+    )
+
+
+def tile_routed_moe_kernel(tc, xT, w_words, w_scales, b, gate, offs, pos1, pos2, out):
+    nc = tc.nc
+    with ExitStack() as ctx:
+        keep = ctx.enter_context(tc.tile_pool(name="keep", bufs=1))
+        psum = ctx.enter_context(tc.psum_pool(name="psum", bufs=1))
+
+        offs_sb = keep.tile([P, SLOTS // 16], U16, name="offs_sb")
+        pos1_sb = keep.tile([P, T // 16], U16, name="pos1_sb")
+        pos2_sb = keep.tile([P, T // 16], U16, name="pos2_sb")
+
+        raw = [keep.tile([P, 4, T], F32, name=f"raw{a}") for a in range(PASSES)]
+        grouped = [keep.tile([P, T, 4], BF16, name=f"grouped{a}", align_bytes=64) for a in range(PASSES)]
+        words = [keep.tile([P, WORD_COLUMNS[a]], I32, name=f"words{a}", align_bytes=64) for a in range(PASSES)]
+        scales = keep.tile([P, SCALE_COLUMNS], U8, name="scales", align_bytes=64)
+        slot_words = [keep.tile([P, SLOTS], U32, name=f"slot_words{a}", align_bytes=64) for a in range(PASSES)]
+        slot_scales = keep.tile([P, SLOTS], U8, name="slot_scales", align_bytes=64)
+        wq = [keep.tile([P, E * N], U32, name=f"wq{a}", align_bytes=64) for a in range(PASSES)]
+        wq_scales = keep.tile([P, E * PASSES * N], U8, name="wq_scales", align_bytes=64)
+        bias = keep.tile([P, E], F32, name="bias")
+        gates = keep.tile([P, 2, T], F32, name="gates")
+        y = keep.tile([P, SLOTS], F32, name="y")
+        part1 = keep.tile([P, T], F32, name="part1")
+        part2 = keep.tile([P, T], F32, name="part2")
+        total = keep.tile([P, T], F32, name="total")
+        warm = keep.tile([P, 1], F32, name="warm")
+
+        def load_x(a):
+            rows = xT[512 * a : 512 * (a + 1), :].rearrange("(p j) w -> p j w", j=4)
+            for lo, hi in LOADS[a]:
+                nc.sync.dma_start(out=raw[a][:, :, lo:hi], in_=rows[:, :, lo:hi])
+
+        load_x(0)
+        nc.sync.dma_start(offs_sb[:], offs)
+        load_x(1)
+        load_x(2)
+
+        nc.scalar.dma_start(out=bias[:], in_=b)
+        nc.gpsimd.memset(warm[:], 0.0)
+        nc.scalar.activation(out=warm[:], in_=warm[:], func=IDENTITY)
+        nc.vector.memset(scales[:].bitcast(I32), 0)
+        nc.vector.memset(words[0][:, T:], 0)
+        nc.vector.memset(words[1][:, T:], 0)
+        nc.vector.memset(wq_scales[:].bitcast(I32), 0)
+
+        def load_w(a):
+            nc.sync.dma_start(
+                out=wq[a][:].bitcast(I32).rearrange("p (e n) -> p e n", e=E),
+                in_=w_words[:, a].rearrange("e p n r -> p e (n r)").bitcast(I32),
+            )
+
+        load_w(0)
+        for q in range(4):
+            nc.sync.dma_start(
+                out=wq_scales[32 * q : 32 * q + 4, :].bitcast(I32).rearrange("r (g n) -> r g n", g=E * PASSES),
+                in_=w_scales[:, :, 4 * q : 4 * q + 4, :].bitcast(I32).rearrange("e a r n -> r (e a) n"),
+            )
+        load_w(1)
+        load_w(2)
+        nc.sync.dma_start(pos1_sb[:], pos1)
+        nc.sync.dma_start(pos2_sb[:], pos2)
+        nc.sync.dma_start(out=gates[:], in_=gate.rearrange("g p t -> p g t"))
+
+        acc = [psum.tile([P, C], F32, name=f"acc{e}") for e in range(E)]
+
+        def multiply(a, e):
+            slots = slice(e * C, (e + 1) * C)
+            weight = slice((e * PASSES + a) * N, (e * PASSES + a + 1) * N)
+            nc.tensor.matmul_mx(
+                out=acc[e][:],
+                lhsT=wq[a][:, e * N : (e + 1) * N].bitcast(FP8X4),
+                lhsT_scale=wq_scales[:, weight],
+                rhs=slot_words[a][:, slots].bitcast(FP8X4),
+                rhs_scale=slot_scales[4 * a : P, slots],
+                start=(a == 0),
+                stop=(a == PASSES - 1),
+            )
+
+        def quantize(a, lo, hi):
+            nc.vector.quantize_mx(
+                out=words[a][:, lo:hi].bitcast(FP8X4),
+                scales=scales[4 * a : P, lo:hi],
+                in_=grouped[a][:, lo:hi, :].rearrange("p t j -> p (t j)"),
+            )
+
+        def gather_words(a, lo, hi):
+            nc.vector.tensor_copy(
+                out=slot_words[a][:, lo:hi],
+                in_=words[a][:].bitcast(U32).indirect(offs_sb[:, lo // 16 : hi // 16]),
+            )
+
+        for a in range(PASSES):
+            for (lo, hi), share in zip(HALVES, VECTOR_TOKENS[a]):
+                cut = lo + share
+                if lo < cut:
+                    interleave(nc.vector.tensor_copy, grouped[a], raw[a], lo, cut)
+                if cut < hi:
+                    interleave(nc.scalar.copy, grouped[a], raw[a], cut, hi)
+                if a < PASSES - 1:
+                    quantize(a, lo, hi)
+            if a < PASSES - 1:
+                gather_words(a, 0, SLOTS)
+            else:
+                quantize(a, 0, T)
+
+        for lo, hi in zip(SCALE_CUTS[:-1], SCALE_CUTS[1:]):
+            nc.vector.tensor_copy(out=slot_scales[:, lo:hi], in_=scales[:].indirect(offs_sb[:, lo // 16 : hi // 16]))
+            for e in range(lo // C, hi // C):
+                for a in range(PASSES - 1):
+                    multiply(a, e)
+        for lo, hi in zip(LAST_CUTS[:-1], LAST_CUTS[1:]):
+            gather_words(PASSES - 1, lo, hi)
+            for e in range(lo // C, hi // C):
+                multiply(PASSES - 1, e)
+                cols = slice(e * C, (e + 1) * C)
+                if e < E - 2:
+                    nc.scalar.activation(out=y[:, cols], in_=acc[e][:], func=IDENTITY, bias=bias[:, e : e + 1])
+                else:
+                    nc.vector.tensor_scalar(out=y[:, cols], in0=acc[e][:], scalar1=bias[:, e : e + 1], scalar2=None, op0=ADD)
+
+        nc.vector.tensor_tensor(out=part1[:], in0=y[:].indirect(pos1_sb[:]), in1=gates[:, 0, :], op=MULT)
+        for lo, hi in HALVES:
+            nc.vector.tensor_tensor(
+                out=part2[:, lo:hi],
+                in0=y[:].indirect(pos2_sb[:, lo // 16 : hi // 16]),
+                in1=gates[:, 1, lo:hi],
+                op=MULT,
+            )
+        for lo, hi in HALVES:
+            nc.vector.tensor_tensor(out=total[:, lo:hi], in0=part1[:, lo:hi], in1=part2[:, lo:hi], op=ADD)
+            nc.sync.dma_start(out=out[:, lo:hi], in_=total[:, lo:hi])

@@ -18,13 +18,16 @@ K, T, E, C, N = 1536, 512, 8, 128, 128
 SLOTS = E * C
 PASSES = K // 512
 FLOPS = 2 * K * N * SLOTS
-WORD_COLUMNS = (1376, 1376, 512)
+WORD_COLUMNS = (1376, 1376, 704)
 SCALE_COLUMNS = 704
 HALVES = ((0, 256), (256, 512))
-VECTOR_TOKENS = ((128, 128), (0, 0), (0, 0))
-LOADS = (((0, 512),), HALVES, HALVES)
-SCALE_CUTS = (0, 512, 1024)
-LAST_CUTS = (0, 384, 768, 1024)
+LOADS = (((0, 512),), ((0, 512),), ((0, 512),))
+VECTOR_COPIES = (((0, 256), (256, 320)), ((0, 64),), ())
+SCALAR_COPIES = (((320, 512),), ((64, 256), (256, 512)), HALVES)
+QUANTIZE_CUTS = (HALVES, HALVES, HALVES)
+WEIGHT_GROUPS = ((0, 2), (2, 4), (4, 6), (6, 8))
+LAST_STEPS = (("scales", 0, 512), ("words", 0, 512), ("scales", 512, 1024), ("words", 512, 896), ("words", 896, 1024))
+VECTOR_BANKS = 1
 
 
 def interleave(copy, grouped, raw, lo, hi):
@@ -50,7 +53,7 @@ def tile_routed_moe_kernel(tc, xT, w_words, w_scales, b, gate, offs, pos1, pos2,
         scales = keep.tile([P, SCALE_COLUMNS], U8, name="scales", align_bytes=64)
         slot_words = [keep.tile([P, SLOTS], U32, name=f"slot_words{a}", align_bytes=64) for a in range(PASSES)]
         slot_scales = keep.tile([P, SLOTS], U8, name="slot_scales", align_bytes=64)
-        wq = [keep.tile([P, E * N], U32, name=f"wq{a}", align_bytes=64) for a in range(PASSES)]
+        wq = keep.tile([P, E * PASSES * N], U32, name="wq", align_bytes=64)
         wq_scales = keep.tile([P, E * PASSES * N], U8, name="wq_scales", align_bytes=64)
         bias = keep.tile([P, E], F32, name="bias")
         gates = keep.tile([P, 2, T], F32, name="gates")
@@ -73,28 +76,26 @@ def tile_routed_moe_kernel(tc, xT, w_words, w_scales, b, gate, offs, pos1, pos2,
         nc.scalar.dma_start(out=bias[:], in_=b)
         nc.gpsimd.memset(warm[:], 0.0)
         nc.scalar.activation(out=warm[:], in_=warm[:], func=IDENTITY)
-        nc.vector.memset(scales[:].bitcast(I32), 0)
-        nc.vector.memset(words[0][:, T:], 0)
-        nc.vector.memset(words[1][:, T:], 0)
         nc.vector.memset(wq_scales[:].bitcast(I32), 0)
+        nc.vector.memset(scales[:].bitcast(I32), 0)
+        for a in range(PASSES):
+            if WORD_COLUMNS[a] > T:
+                nc.vector.memset(words[a][:, T:], 0)
 
-        def load_w(a):
-            nc.sync.dma_start(
-                out=wq[a][:].bitcast(I32).rearrange("p (e n) -> p e n", e=E),
-                in_=w_words[:, a].rearrange("e p n r -> p e (n r)").bitcast(I32),
-            )
-
-        load_w(0)
         for q in range(4):
             nc.sync.dma_start(
                 out=wq_scales[32 * q : 32 * q + 4, :].bitcast(I32).rearrange("r (g n) -> r g n", g=E * PASSES),
                 in_=w_scales[:, :, 4 * q : 4 * q + 4, :].bitcast(I32).rearrange("e a r n -> r (e a) n"),
             )
-        load_w(1)
-        load_w(2)
+        for lo, hi in WEIGHT_GROUPS:
+            nc.sync.dma_start(
+                out=wq[:, lo * PASSES * N : hi * PASSES * N].bitcast(I32).rearrange("p (g n) -> p g n", n=N),
+                in_=w_words[lo:hi].rearrange("e a p n r -> p (e a) (n r)").bitcast(I32),
+            )
         nc.sync.dma_start(pos1_sb[:], pos1)
         nc.sync.dma_start(pos2_sb[:], pos2)
-        nc.sync.dma_start(out=gates[:], in_=gate.rearrange("g p t -> p g t"))
+        for g in range(2):
+            nc.sync.dma_start(out=gates[:, g, :], in_=gate[g])
 
         acc = [psum.tile([P, C], F32, name=f"acc{e}") for e in range(E)]
 
@@ -103,7 +104,7 @@ def tile_routed_moe_kernel(tc, xT, w_words, w_scales, b, gate, offs, pos1, pos2,
             weight = slice((e * PASSES + a) * N, (e * PASSES + a + 1) * N)
             nc.tensor.matmul_mx(
                 out=acc[e][:],
-                lhsT=wq[a][:, e * N : (e + 1) * N].bitcast(FP8X4),
+                lhsT=wq[:, weight].bitcast(FP8X4),
                 lhsT_scale=wq_scales[:, weight],
                 rhs=slot_words[a][:, slots].bitcast(FP8X4),
                 rhs_scale=slot_scales[4 * a : P, slots],
@@ -125,33 +126,31 @@ def tile_routed_moe_kernel(tc, xT, w_words, w_scales, b, gate, offs, pos1, pos2,
             )
 
         for a in range(PASSES):
-            for (lo, hi), share in zip(HALVES, VECTOR_TOKENS[a]):
-                cut = lo + share
-                if lo < cut:
-                    interleave(nc.vector.tensor_copy, grouped[a], raw[a], lo, cut)
-                if cut < hi:
-                    interleave(nc.scalar.copy, grouped[a], raw[a], cut, hi)
-                if a < PASSES - 1:
-                    quantize(a, lo, hi)
+            for lo, hi in VECTOR_COPIES[a]:
+                interleave(nc.vector.tensor_copy, grouped[a], raw[a], lo, hi)
+            for lo, hi in SCALAR_COPIES[a]:
+                interleave(nc.scalar.copy, grouped[a], raw[a], lo, hi)
+            for lo, hi in QUANTIZE_CUTS[a]:
+                quantize(a, lo, hi)
             if a < PASSES - 1:
                 gather_words(a, 0, SLOTS)
-            else:
-                quantize(a, 0, T)
 
-        for lo, hi in zip(SCALE_CUTS[:-1], SCALE_CUTS[1:]):
-            nc.vector.tensor_copy(out=slot_scales[:, lo:hi], in_=scales[:].indirect(offs_sb[:, lo // 16 : hi // 16]))
-            for e in range(lo // C, hi // C):
-                for a in range(PASSES - 1):
-                    multiply(a, e)
-        for lo, hi in zip(LAST_CUTS[:-1], LAST_CUTS[1:]):
-            gather_words(PASSES - 1, lo, hi)
-            for e in range(lo // C, hi // C):
-                multiply(PASSES - 1, e)
-                cols = slice(e * C, (e + 1) * C)
-                if e < E - 2:
-                    nc.scalar.activation(out=y[:, cols], in_=acc[e][:], func=IDENTITY, bias=bias[:, e : e + 1])
-                else:
-                    nc.vector.tensor_scalar(out=y[:, cols], in0=acc[e][:], scalar1=bias[:, e : e + 1], scalar2=None, op0=ADD)
+        for kind, lo, hi in LAST_STEPS:
+            experts = range(lo // C, hi // C)
+            if kind == "scales":
+                nc.vector.tensor_copy(out=slot_scales[:, lo:hi], in_=scales[:].indirect(offs_sb[:, lo // 16 : hi // 16]))
+                for e in experts:
+                    for a in range(PASSES - 1):
+                        multiply(a, e)
+            else:
+                gather_words(PASSES - 1, lo, hi)
+                for e in experts:
+                    multiply(PASSES - 1, e)
+                    cols = slice(e * C, (e + 1) * C)
+                    if e < E - VECTOR_BANKS:
+                        nc.scalar.activation(out=y[:, cols], in_=acc[e][:], func=IDENTITY, bias=bias[:, e : e + 1])
+                    else:
+                        nc.vector.tensor_scalar(out=y[:, cols], in0=acc[e][:], scalar1=bias[:, e : e + 1], scalar2=None, op0=ADD)
 
         nc.vector.tensor_tensor(out=part1[:], in0=y[:].indirect(pos1_sb[:]), in1=gates[:, 0, :], op=MULT)
         for lo, hi in HALVES:

@@ -18,16 +18,20 @@ K, T, E, C, N = 1536, 512, 8, 128, 128
 SLOTS = E * C
 PASSES = K // 512
 FLOPS = 2 * K * N * SLOTS
-WORD_COLUMNS = (1376, 1376, 704)
+WORD_COLUMNS = (1120, 1120, 704)
 SCALE_COLUMNS = 704
 HALVES = ((0, 256), (256, 512))
 LOADS = (((0, 512),), ((0, 512),), ((0, 512),))
-VECTOR_COPIES = (((0, 256), (256, 320)), ((0, 64),), ())
-SCALAR_COPIES = (((320, 512),), ((64, 256), (256, 512)), HALVES)
+VECTOR_COPIES = ((), (), ())
+SCALAR_COPIES = ((), ((0, 256), (256, 384)), ((0, 256), (256, 384)))
 QUANTIZE_CUTS = (HALVES, HALVES, HALVES)
-WEIGHT_GROUPS = ((0, 2), (2, 4), (4, 6), (6, 8))
-LAST_STEPS = (("scales", 0, 512), ("words", 0, 512), ("scales", 512, 1024), ("words", 512, 896), ("words", 896, 1024))
-VECTOR_BANKS = 1
+WEIGHT_GROUPS = ((0, 3), (3, 6), (6, 7), (7, 8))
+LAST_STEPS = (("scales", 0, 384), ("words", 0, 384), ("scales", 384, 768), ("words", 384, 768), ("scales", 768, 1024), ("words", 768, 896), ("words", 896, 1024))
+FIRST_SLOTS = 832
+PAIR_VECTOR = (((0, 320),), ((0, 256), (256, 320)))
+PAIR_SCALAR = (((320, 512),), ((320, 512),))
+GPSIMD_COPIES = ((), ((384, 512),), ((384, 512),))
+VECTOR_BANKS = 2
 
 
 def interleave(copy, grouped, raw, lo, hi):
@@ -35,6 +39,10 @@ def interleave(copy, grouped, raw, lo, hi):
         out=grouped[:, lo:hi, :].rearrange("p (c i) j -> p c j i", i=4),
         in_=raw[:, :, lo:hi].rearrange("p j (c i) -> p c j i", i=4),
     )
+
+
+def interleave_pair(copy, grouped, raw, u, lo, hi):
+    copy(out=grouped[:, lo:hi, 2 * u : 2 * u + 2], in_=raw[:, 2 * u : 2 * u + 2, lo:hi].rearrange("p j t -> p t j"))
 
 
 def tile_routed_moe_kernel(tc, xT, w_words, w_scales, b, gate, offs, pos1, pos2, out):
@@ -68,7 +76,9 @@ def tile_routed_moe_kernel(tc, xT, w_words, w_scales, b, gate, offs, pos1, pos2,
             for lo, hi in LOADS[a]:
                 nc.sync.dma_start(out=raw[a][:, :, lo:hi], in_=rows[:, :, lo:hi])
 
-        load_x(0)
+        first_rows = xT[0:512, :].rearrange("(p j) w -> p j w", j=4)
+        for u in range(2):
+            nc.sync.dma_start(out=raw[0][:, 2 * u : 2 * u + 2, :], in_=first_rows[:, 2 * u : 2 * u + 2, :])
         nc.sync.dma_start(offs_sb[:], offs)
         load_x(1)
         load_x(2)
@@ -125,15 +135,25 @@ def tile_routed_moe_kernel(tc, xT, w_words, w_scales, b, gate, offs, pos1, pos2,
                 in_=words[a][:].bitcast(U32).indirect(offs_sb[:, lo // 16 : hi // 16]),
             )
 
+        for u in range(2):
+            for lo, hi in PAIR_VECTOR[u]:
+                interleave_pair(nc.vector.tensor_copy, grouped[0], raw[0], u, lo, hi)
+            for lo, hi in PAIR_SCALAR[u]:
+                interleave_pair(nc.scalar.copy, grouped[0], raw[0], u, lo, hi)
+
         for a in range(PASSES):
             for lo, hi in VECTOR_COPIES[a]:
                 interleave(nc.vector.tensor_copy, grouped[a], raw[a], lo, hi)
+            for lo, hi in GPSIMD_COPIES[a]:
+                interleave(nc.gpsimd.tensor_copy, grouped[a], raw[a], lo, hi)
             for lo, hi in SCALAR_COPIES[a]:
                 interleave(nc.scalar.copy, grouped[a], raw[a], lo, hi)
             for lo, hi in QUANTIZE_CUTS[a]:
                 quantize(a, lo, hi)
+            if a > 0 and FIRST_SLOTS < SLOTS:
+                gather_words(a - 1, FIRST_SLOTS, SLOTS)
             if a < PASSES - 1:
-                gather_words(a, 0, SLOTS)
+                gather_words(a, 0, FIRST_SLOTS)
 
         for kind, lo, hi in LAST_STEPS:
             experts = range(lo // C, hi // C)

@@ -18,19 +18,20 @@ K, T, E, C, N = 1536, 512, 8, 128, 128
 SLOTS = E * C
 PASSES = K // 512
 FLOPS = 2 * K * N * SLOTS
-WORD_COLUMNS = (1120, 1120, 704)
+WORD_COLUMNS = (1200, 1200, 512)
 SCALE_COLUMNS = 704
 HALVES = ((0, 256), (256, 512))
 LOADS = (((0, 512),), ((0, 512),), ((0, 512),))
 VECTOR_COPIES = ((), (), ())
-SCALAR_COPIES = ((), ((0, 256), (256, 384)), ((0, 256), (256, 384)))
-QUANTIZE_CUTS = (HALVES, HALVES, HALVES)
+SCALAR_COPIES = ((), (), ((0, 288),))
+QUANTIZE_CUTS = (HALVES, ((0, 512),), ((0, 512),))
 WEIGHT_GROUPS = ((0, 3), (3, 6), (6, 7), (7, 8))
 LAST_STEPS = (("scales", 0, 384), ("words", 0, 384), ("scales", 384, 768), ("words", 384, 768), ("scales", 768, 1024), ("words", 768, 896), ("words", 896, 1024))
-FIRST_SLOTS = 832
+FIRST_SLOTS = 896
 PAIR_VECTOR = (((0, 320),), ((0, 256), (256, 320)))
 PAIR_SCALAR = (((320, 512),), ((320, 512),))
-GPSIMD_COPIES = ((), ((384, 512),), ((384, 512),))
+GPSIMD_COPIES = ((), ((352, 512),), ((288, 512),))
+NARROW_OFFSETS = 384
 VECTOR_BANKS = 2
 
 
@@ -69,7 +70,6 @@ def tile_routed_moe_kernel(tc, xT, w_words, w_scales, b, gate, offs, pos1, pos2,
         part1 = keep.tile([P, T], F32, name="part1")
         part2 = keep.tile([P, T], F32, name="part2")
         total = keep.tile([P, T], F32, name="total")
-        warm = keep.tile([P, 1], F32, name="warm")
 
         def load_x(a):
             rows = xT[512 * a : 512 * (a + 1), :].rearrange("(p j) w -> p j w", j=4)
@@ -80,12 +80,11 @@ def tile_routed_moe_kernel(tc, xT, w_words, w_scales, b, gate, offs, pos1, pos2,
         for u in range(2):
             nc.sync.dma_start(out=raw[0][:, 2 * u : 2 * u + 2, :], in_=first_rows[:, 2 * u : 2 * u + 2, :])
         nc.sync.dma_start(offs_sb[:], offs)
-        load_x(1)
+        second_rows = xT[512:1024, :].rearrange("(p j) w -> p j w", j=4)
+        for u in range(2):
+            nc.sync.dma_start(out=raw[1][:, 2 * u : 2 * u + 2, :], in_=second_rows[:, 2 * u : 2 * u + 2, :])
         load_x(2)
 
-        nc.scalar.dma_start(out=bias[:], in_=b)
-        nc.gpsimd.memset(warm[:], 0.0)
-        nc.scalar.activation(out=warm[:], in_=warm[:], func=IDENTITY)
         nc.vector.memset(wq_scales[:].bitcast(I32), 0)
         nc.vector.memset(scales[:].bitcast(I32), 0)
         for a in range(PASSES):
@@ -97,6 +96,7 @@ def tile_routed_moe_kernel(tc, xT, w_words, w_scales, b, gate, offs, pos1, pos2,
                 out=wq_scales[32 * q : 32 * q + 4, :].bitcast(I32).rearrange("r (g n) -> r g n", g=E * PASSES),
                 in_=w_scales[:, :, 4 * q : 4 * q + 4, :].bitcast(I32).rearrange("e a r n -> r (e a) n"),
             )
+        nc.sync.dma_start(out=bias[:], in_=b)
         for lo, hi in WEIGHT_GROUPS:
             nc.sync.dma_start(
                 out=wq[:, lo * PASSES * N : hi * PASSES * N].bitcast(I32).rearrange("p (g n) -> p g n", n=N),
@@ -130,9 +130,10 @@ def tile_routed_moe_kernel(tc, xT, w_words, w_scales, b, gate, offs, pos1, pos2,
             )
 
         def gather_words(a, lo, hi):
+            window = words[a][:] if hi - lo > NARROW_OFFSETS else words[a][:, :T]
             nc.vector.tensor_copy(
                 out=slot_words[a][:, lo:hi],
-                in_=words[a][:].bitcast(U32).indirect(offs_sb[:, lo // 16 : hi // 16]),
+                in_=window.bitcast(U32).indirect(offs_sb[:, lo // 16 : hi // 16]),
             )
 
         for u in range(2):
@@ -142,10 +143,13 @@ def tile_routed_moe_kernel(tc, xT, w_words, w_scales, b, gate, offs, pos1, pos2,
                 interleave_pair(nc.scalar.copy, grouped[0], raw[0], u, lo, hi)
 
         for a in range(PASSES):
+            if a == 1:
+                for u in range(2):
+                    interleave_pair(nc.scalar.copy, grouped[1], raw[1], u, 0, 352)
             for lo, hi in VECTOR_COPIES[a]:
                 interleave(nc.vector.tensor_copy, grouped[a], raw[a], lo, hi)
             for lo, hi in GPSIMD_COPIES[a]:
-                interleave(nc.gpsimd.tensor_copy, grouped[a], raw[a], lo, hi)
+                nc.gpsimd.tensor_copy(out=grouped[a][:, lo:hi, :], in_=raw[a][:, :, lo:hi].rearrange("p j t -> p t j"))
             for lo, hi in SCALAR_COPIES[a]:
                 interleave(nc.scalar.copy, grouped[a], raw[a], lo, hi)
             for lo, hi in QUANTIZE_CUTS[a]:

@@ -28,9 +28,9 @@ QUANTIZE_CUTS = (HALVES, ((0, 512),), ((0, 512),))
 WEIGHT_GROUPS = ((0, 3), (3, 6), (6, 7), (7, 8))
 LAST_STEPS = (("scales", 0, 384), ("words", 0, 384), ("scales", 384, 768), ("words", 384, 768), ("scales", 768, 1024), ("words", 768, 896), ("words", 896, 1024))
 FIRST_SLOTS = 896
-PAIR_VECTOR = (((0, 320),), ((0, 256), (256, 320)))
-PAIR_SCALAR = (((320, 512),), ((320, 512),))
-GPSIMD_COPIES = ((), ((352, 512),), ((288, 512),))
+PAIR_VECTOR = (((0, 384),), ((0, 256), (256, 384)))
+PAIR_SCALAR = (((384, 512),), ((384, 512),))
+GPSIMD_COPIES = ((), ((320, 512),), ((288, 512),))
 NARROW_OFFSETS = 384
 VECTOR_BANKS = 2
 
@@ -145,7 +145,7 @@ def tile_routed_moe_kernel(tc, xT, w_words, w_scales, b, gate, offs, pos1, pos2,
         for a in range(PASSES):
             if a == 1:
                 for u in range(2):
-                    interleave_pair(nc.scalar.copy, grouped[1], raw[1], u, 0, 352)
+                    interleave_pair(nc.scalar.copy, grouped[1], raw[1], u, 0, 320)
             for lo, hi in VECTOR_COPIES[a]:
                 interleave(nc.vector.tensor_copy, grouped[a], raw[a], lo, hi)
             for lo, hi in GPSIMD_COPIES[a]:
@@ -176,14 +176,22 @@ def tile_routed_moe_kernel(tc, xT, w_words, w_scales, b, gate, offs, pos1, pos2,
                     else:
                         nc.vector.tensor_scalar(out=y[:, cols], in0=acc[e][:], scalar1=bias[:, e : e + 1], scalar2=None, op0=ADD)
 
-        nc.vector.tensor_tensor(out=part1[:], in0=y[:].indirect(pos1_sb[:]), in1=gates[:, 0, :], op=MULT)
-        for lo, hi in HALVES:
+        def second_product(lo, hi):
             nc.vector.tensor_tensor(
                 out=part2[:, lo:hi],
                 in0=y[:].indirect(pos2_sb[:, lo // 16 : hi // 16]),
                 in1=gates[:, 1, lo:hi],
                 op=MULT,
             )
-        for lo, hi in HALVES:
+
+        def add_and_store(lo, hi):
             nc.vector.tensor_tensor(out=total[:, lo:hi], in0=part1[:, lo:hi], in1=part2[:, lo:hi], op=ADD)
             nc.sync.dma_start(out=out[:, lo:hi], in_=total[:, lo:hi])
+
+        nc.vector.tensor_tensor(out=part1[:], in0=y[:].indirect(pos1_sb[:]), in1=gates[:, 0, :], op=MULT)
+        second_product(0, 256)
+        second_product(256, 384)
+        add_and_store(0, 256)
+        second_product(384, 512)
+        add_and_store(256, 384)
+        add_and_store(384, 512)

@@ -17,33 +17,17 @@ P = 128
 K, T, E, C, N = 1536, 512, 8, 128, 128
 SLOTS = E * C
 PASSES = K // 512
+LAST = PASSES - 1
 FLOPS = 2 * K * N * SLOTS
-WORD_COLUMNS = (1200, 1200, 512)
-SCALE_COLUMNS = 704
-HALVES = ((0, 256), (256, 512))
-LOADS = (((0, 512),), ((0, 512),), ((0, 512),))
-VECTOR_COPIES = ((), (), ())
-SCALAR_COPIES = ((), (), ((0, 288),))
-QUANTIZE_CUTS = (HALVES, ((0, 512),), ((0, 512),))
-WEIGHT_GROUPS = ((0, 3), (3, 6), (6, 7), (7, 8))
-LAST_STEPS = (("scales", 0, 384), ("words", 0, 384), ("scales", 384, 768), ("words", 384, 768), ("scales", 768, 1024), ("words", 768, 896), ("words", 896, 1024))
-FIRST_SLOTS = 896
-PAIR_VECTOR = (((0, 384),), ((0, 256), (256, 384)))
-PAIR_SCALAR = (((384, 512),), ((384, 512),))
-GPSIMD_COPIES = ((), ((320, 512),), ((288, 512),))
-NARROW_OFFSETS = 384
-VECTOR_BANKS = 2
+HALF = T // 2
+QUARTER = T // 4
 
-
-def interleave(copy, grouped, raw, lo, hi):
-    copy(
-        out=grouped[:, lo:hi, :].rearrange("p (c i) j -> p c j i", i=4),
-        in_=raw[:, :, lo:hi].rearrange("p j (c i) -> p c j i", i=4),
-    )
-
-
-def interleave_pair(copy, grouped, raw, u, lo, hi):
-    copy(out=grouped[:, lo:hi, 2 * u : 2 * u + 2], in_=raw[:, 2 * u : 2 * u + 2, lo:hi].rearrange("p j t -> p t j"))
+WIDE_COLUMNS = 1376
+SCALAR_FROM = 3 * QUARTER
+GPSIMD_FROM = (None, 320, 288)
+WEIGHT_LOADS = ((0, 3), (3, 6), (6, 7), (7, 8))
+EXPERT_GROUPS = ((0, 3), (3, 6), (6, 8))
+VECTOR_BANKS_FROM = 6
 
 
 def tile_routed_moe_kernel(tc, xT, w_words, w_scales, b, gate, offs, pos1, pos2, out):
@@ -58,8 +42,8 @@ def tile_routed_moe_kernel(tc, xT, w_words, w_scales, b, gate, offs, pos1, pos2,
 
         raw = [keep.tile([P, 4, T], F32, name=f"raw{a}") for a in range(PASSES)]
         grouped = [keep.tile([P, T, 4], BF16, name=f"grouped{a}", align_bytes=64) for a in range(PASSES)]
-        words = [keep.tile([P, WORD_COLUMNS[a]], I32, name=f"words{a}", align_bytes=64) for a in range(PASSES)]
-        scales = keep.tile([P, SCALE_COLUMNS], U8, name="scales", align_bytes=64)
+        words = [keep.tile([P, T if a == LAST else WIDE_COLUMNS], I32, name=f"words{a}", align_bytes=64) for a in range(PASSES)]
+        scales = keep.tile([P, T], U8, name="scales", align_bytes=64)
         slot_words = [keep.tile([P, SLOTS], U32, name=f"slot_words{a}", align_bytes=64) for a in range(PASSES)]
         slot_scales = keep.tile([P, SLOTS], U8, name="slot_scales", align_bytes=64)
         wq = keep.tile([P, E * PASSES * N], U32, name="wq", align_bytes=64)
@@ -70,26 +54,23 @@ def tile_routed_moe_kernel(tc, xT, w_words, w_scales, b, gate, offs, pos1, pos2,
         part1 = keep.tile([P, T], F32, name="part1")
         part2 = keep.tile([P, T], F32, name="part2")
         total = keep.tile([P, T], F32, name="total")
+        acc = [psum.tile([P, C], F32, name=f"acc{e}") for e in range(E)]
 
-        def load_x(a):
-            rows = xT[512 * a : 512 * (a + 1), :].rearrange("(p j) w -> p j w", j=4)
-            for lo, hi in LOADS[a]:
-                nc.sync.dma_start(out=raw[a][:, :, lo:hi], in_=rows[:, :, lo:hi])
+        def load_x(a, first, count):
+            rows = xT[512 * a : 512 * (a + 1), :].rearrange("(p j) t -> p j t", j=4)
+            nc.sync.dma_start(out=raw[a][:, first : first + count, :], in_=rows[:, first : first + count, :])
 
-        first_rows = xT[0:512, :].rearrange("(p j) w -> p j w", j=4)
-        for u in range(2):
-            nc.sync.dma_start(out=raw[0][:, 2 * u : 2 * u + 2, :], in_=first_rows[:, 2 * u : 2 * u + 2, :])
+        load_x(0, 0, 2)
+        load_x(0, 2, 2)
         nc.sync.dma_start(offs_sb[:], offs)
-        second_rows = xT[512:1024, :].rearrange("(p j) w -> p j w", j=4)
-        for u in range(2):
-            nc.sync.dma_start(out=raw[1][:, 2 * u : 2 * u + 2, :], in_=second_rows[:, 2 * u : 2 * u + 2, :])
-        load_x(2)
+        load_x(1, 0, 2)
+        load_x(1, 2, 2)
+        load_x(2, 0, 4)
 
         nc.vector.memset(wq_scales[:].bitcast(I32), 0)
         nc.vector.memset(scales[:].bitcast(I32), 0)
-        for a in range(PASSES):
-            if WORD_COLUMNS[a] > T:
-                nc.vector.memset(words[a][:, T:], 0)
+        for a in range(LAST):
+            nc.vector.memset(words[a][:, T:], 0)
 
         for q in range(4):
             nc.sync.dma_start(
@@ -97,7 +78,7 @@ def tile_routed_moe_kernel(tc, xT, w_words, w_scales, b, gate, offs, pos1, pos2,
                 in_=w_scales[:, :, 4 * q : 4 * q + 4, :].bitcast(I32).rearrange("e a r n -> r (e a) n"),
             )
         nc.sync.dma_start(out=bias[:], in_=b)
-        for lo, hi in WEIGHT_GROUPS:
+        for lo, hi in WEIGHT_LOADS:
             nc.sync.dma_start(
                 out=wq[:, lo * PASSES * N : hi * PASSES * N].bitcast(I32).rearrange("p (g n) -> p g n", n=N),
                 in_=w_words[lo:hi].rearrange("e a p n r -> p (e a) (n r)").bitcast(I32),
@@ -107,7 +88,25 @@ def tile_routed_moe_kernel(tc, xT, w_words, w_scales, b, gate, offs, pos1, pos2,
         for g in range(2):
             nc.sync.dma_start(out=gates[:, g, :], in_=gate[g])
 
-        acc = [psum.tile([P, C], F32, name=f"acc{e}") for e in range(E)]
+        def round_pair(copy, a, first, lo, hi):
+            copy(out=grouped[a][:, lo:hi, first : first + 2], in_=raw[a][:, first : first + 2, lo:hi].rearrange("p j t -> p t j"))
+
+        def round_on_gpsimd(a):
+            lo = GPSIMD_FROM[a]
+            nc.gpsimd.tensor_copy(out=grouped[a][:, lo:, :], in_=raw[a][:, :, lo:].rearrange("p j t -> p t j"))
+
+        def quantize(a, lo, hi):
+            nc.vector.quantize_mx(
+                out=words[a][:, lo:hi].bitcast(FP8X4),
+                scales=scales[4 * a : P, lo:hi],
+                in_=grouped[a][:, lo:hi, :].rearrange("p t j -> p (t j)"),
+            )
+
+        def gather_words(a, lo, hi):
+            nc.vector.tensor_copy(
+                out=slot_words[a][:, lo:hi],
+                in_=words[a][:].bitcast(U32).indirect(offs_sb[:, lo // 16 : hi // 16]),
+            )
 
         def multiply(a, e):
             slots = slice(e * C, (e + 1) * C)
@@ -119,62 +118,54 @@ def tile_routed_moe_kernel(tc, xT, w_words, w_scales, b, gate, offs, pos1, pos2,
                 rhs=slot_words[a][:, slots].bitcast(FP8X4),
                 rhs_scale=slot_scales[4 * a : P, slots],
                 start=(a == 0),
-                stop=(a == PASSES - 1),
+                stop=(a == LAST),
             )
 
-        def quantize(a, lo, hi):
-            nc.vector.quantize_mx(
-                out=words[a][:, lo:hi].bitcast(FP8X4),
-                scales=scales[4 * a : P, lo:hi],
-                in_=grouped[a][:, lo:hi, :].rearrange("p t j -> p (t j)"),
-            )
+        def finish(lo, hi):
+            gather_words(LAST, lo * C, hi * C)
+            for e in range(lo, hi):
+                multiply(LAST, e)
+                cols = slice(e * C, (e + 1) * C)
+                if e < VECTOR_BANKS_FROM:
+                    nc.scalar.activation(out=y[:, cols], in_=acc[e][:], func=IDENTITY, bias=bias[:, e : e + 1])
+                else:
+                    nc.vector.tensor_scalar(out=y[:, cols], in0=acc[e][:], scalar1=bias[:, e : e + 1], scalar2=None, op0=ADD)
 
-        def gather_words(a, lo, hi):
-            window = words[a][:] if hi - lo > NARROW_OFFSETS else words[a][:, :T]
+        round_pair(nc.vector.tensor_copy, 0, 0, 0, SCALAR_FROM)
+        round_pair(nc.scalar.copy, 0, 0, SCALAR_FROM, T)
+        round_pair(nc.vector.tensor_copy, 0, 2, 0, HALF)
+        round_pair(nc.vector.tensor_copy, 0, 2, HALF, SCALAR_FROM)
+        round_pair(nc.scalar.copy, 0, 2, SCALAR_FROM, T)
+        quantize(0, 0, HALF)
+        quantize(0, HALF, T)
+        gather_words(0, 0, SLOTS)
+
+        round_pair(nc.scalar.copy, 1, 0, 0, GPSIMD_FROM[1])
+        round_pair(nc.scalar.copy, 1, 2, 0, GPSIMD_FROM[1])
+        round_on_gpsimd(1)
+        quantize(1, 0, T)
+        gather_words(1, 0, SLOTS)
+
+        round_on_gpsimd(LAST)
+        nc.scalar.copy(
+            out=grouped[LAST][:, : GPSIMD_FROM[LAST], :].rearrange("p (c i) j -> p c j i", i=4),
+            in_=raw[LAST][:, :, : GPSIMD_FROM[LAST]].rearrange("p j (c i) -> p c j i", i=4),
+        )
+        quantize(LAST, 0, T)
+
+        for lo, hi in EXPERT_GROUPS:
             nc.vector.tensor_copy(
-                out=slot_words[a][:, lo:hi],
-                in_=window.bitcast(U32).indirect(offs_sb[:, lo // 16 : hi // 16]),
+                out=slot_scales[:, lo * C : hi * C],
+                in_=scales[:].indirect(offs_sb[:, lo * C // 16 : hi * C // 16]),
             )
-
-        for u in range(2):
-            for lo, hi in PAIR_VECTOR[u]:
-                interleave_pair(nc.vector.tensor_copy, grouped[0], raw[0], u, lo, hi)
-            for lo, hi in PAIR_SCALAR[u]:
-                interleave_pair(nc.scalar.copy, grouped[0], raw[0], u, lo, hi)
-
-        for a in range(PASSES):
-            if a == 1:
-                for u in range(2):
-                    interleave_pair(nc.scalar.copy, grouped[1], raw[1], u, 0, 320)
-            for lo, hi in VECTOR_COPIES[a]:
-                interleave(nc.vector.tensor_copy, grouped[a], raw[a], lo, hi)
-            for lo, hi in GPSIMD_COPIES[a]:
-                nc.gpsimd.tensor_copy(out=grouped[a][:, lo:hi, :], in_=raw[a][:, :, lo:hi].rearrange("p j t -> p t j"))
-            for lo, hi in SCALAR_COPIES[a]:
-                interleave(nc.scalar.copy, grouped[a], raw[a], lo, hi)
-            for lo, hi in QUANTIZE_CUTS[a]:
-                quantize(a, lo, hi)
-            if a > 0 and FIRST_SLOTS < SLOTS:
-                gather_words(a - 1, FIRST_SLOTS, SLOTS)
-            if a < PASSES - 1:
-                gather_words(a, 0, FIRST_SLOTS)
-
-        for kind, lo, hi in LAST_STEPS:
-            experts = range(lo // C, hi // C)
-            if kind == "scales":
-                nc.vector.tensor_copy(out=slot_scales[:, lo:hi], in_=scales[:].indirect(offs_sb[:, lo // 16 : hi // 16]))
-                for e in experts:
-                    for a in range(PASSES - 1):
-                        multiply(a, e)
+            for e in range(lo, hi):
+                for a in range(LAST):
+                    multiply(a, e)
+            if hi < E:
+                finish(lo, hi)
             else:
-                gather_words(PASSES - 1, lo, hi)
-                for e in experts:
-                    multiply(PASSES - 1, e)
-                    cols = slice(e * C, (e + 1) * C)
-                    if e < E - VECTOR_BANKS:
-                        nc.scalar.activation(out=y[:, cols], in_=acc[e][:], func=IDENTITY, bias=bias[:, e : e + 1])
-                    else:
-                        nc.vector.tensor_scalar(out=y[:, cols], in0=acc[e][:], scalar1=bias[:, e : e + 1], scalar2=None, op0=ADD)
+                for e in range(lo, hi):
+                    finish(e, e + 1)
 
         def second_product(lo, hi):
             nc.vector.tensor_tensor(
@@ -189,9 +180,9 @@ def tile_routed_moe_kernel(tc, xT, w_words, w_scales, b, gate, offs, pos1, pos2,
             nc.sync.dma_start(out=out[:, lo:hi], in_=total[:, lo:hi])
 
         nc.vector.tensor_tensor(out=part1[:], in0=y[:].indirect(pos1_sb[:]), in1=gates[:, 0, :], op=MULT)
-        second_product(0, 256)
-        second_product(256, 384)
-        add_and_store(0, 256)
-        second_product(384, 512)
-        add_and_store(256, 384)
-        add_and_store(384, 512)
+        second_product(0, HALF)
+        second_product(HALF, HALF + QUARTER)
+        add_and_store(0, HALF)
+        second_product(HALF + QUARTER, T)
+        add_and_store(HALF, HALF + QUARTER)
+        add_and_store(HALF + QUARTER, T)

@@ -42,7 +42,9 @@ def tile_routed_moe_kernel(tc, xT, w_words, w_scales, b, gate, offs, pos1, pos2,
 
         raw = [keep.tile([P, 4, T], F32, name=f"raw{a}") for a in range(PASSES)]
         grouped = [keep.tile([P, T, 4], BF16, name=f"grouped{a}", align_bytes=64) for a in range(PASSES)]
-        words = [keep.tile([P, T if a == LAST else WIDE_COLUMNS], I32, name=f"words{a}", align_bytes=64) for a in range(PASSES)]
+        pitch, reach, ahead = 1152, 1280, 864
+        all_words = keep.tile([P, LAST * pitch + T], I32, name="all_words", align_bytes=64)
+        words = [all_words[:, a * pitch :] for a in range(PASSES)]
         scales = keep.tile([P, T], U8, name="scales", align_bytes=64)
         slot_words = [keep.tile([P, SLOTS], U32, name=f"slot_words{a}", align_bytes=64) for a in range(PASSES)]
         slot_scales = keep.tile([P, SLOTS], U8, name="slot_scales", align_bytes=64)
@@ -67,10 +69,10 @@ def tile_routed_moe_kernel(tc, xT, w_words, w_scales, b, gate, offs, pos1, pos2,
         load_x(1, 2, 2)
         load_x(2, 0, 4)
 
-        nc.vector.memset(wq_scales[:].bitcast(I32), 0)
         nc.vector.memset(scales[:].bitcast(I32), 0)
         for a in range(LAST):
-            nc.vector.memset(words[a][:, T:], 0)
+            nc.vector.memset(words[a][:, T:pitch], 0)
+        nc.gpsimd.memset(wq_scales[:].bitcast(I32), 0)
 
         for q in range(4):
             nc.sync.dma_start(
@@ -102,10 +104,10 @@ def tile_routed_moe_kernel(tc, xT, w_words, w_scales, b, gate, offs, pos1, pos2,
                 in_=grouped[a][:, lo:hi, :].rearrange("p t j -> p (t j)"),
             )
 
-        def gather_words(a, lo, hi):
+        def gather_words(a, lo, hi, width):
             nc.vector.tensor_copy(
                 out=slot_words[a][:, lo:hi],
-                in_=words[a][:].bitcast(U32).indirect(offs_sb[:, lo // 16 : hi // 16]),
+                in_=words[a][:, :width].bitcast(U32).indirect(offs_sb[:, lo // 16 : hi // 16]),
             )
 
         def multiply(a, e):
@@ -122,7 +124,7 @@ def tile_routed_moe_kernel(tc, xT, w_words, w_scales, b, gate, offs, pos1, pos2,
             )
 
         def finish(lo, hi):
-            gather_words(LAST, lo * C, hi * C)
+            gather_words(LAST, lo * C, hi * C, T)
             for e in range(lo, hi):
                 multiply(LAST, e)
                 cols = slice(e * C, (e + 1) * C)
@@ -138,20 +140,24 @@ def tile_routed_moe_kernel(tc, xT, w_words, w_scales, b, gate, offs, pos1, pos2,
         round_pair(nc.scalar.copy, 0, 2, SCALAR_FROM, T)
         quantize(0, 0, HALF)
         quantize(0, HALF, T)
-        gather_words(0, 0, SLOTS)
+        gather_words(0, 0, ahead, pitch)
 
         round_pair(nc.scalar.copy, 1, 0, 0, GPSIMD_FROM[1])
         round_pair(nc.scalar.copy, 1, 2, 0, GPSIMD_FROM[1])
         round_on_gpsimd(1)
-        quantize(1, 0, T)
-        gather_words(1, 0, SLOTS)
+        quantize(1, 0, HALF)
+        quantize(1, HALF, T)
+        gather_words(0, ahead, SLOTS, reach)
+        gather_words(1, 0, ahead, pitch)
 
         round_on_gpsimd(LAST)
         nc.scalar.copy(
             out=grouped[LAST][:, : GPSIMD_FROM[LAST], :].rearrange("p (c i) j -> p c j i", i=4),
             in_=raw[LAST][:, :, : GPSIMD_FROM[LAST]].rearrange("p j (c i) -> p c j i", i=4),
         )
-        quantize(LAST, 0, T)
+        quantize(LAST, 0, HALF)
+        quantize(LAST, HALF, T)
+        gather_words(1, ahead, SLOTS, reach)
 
         for lo, hi in EXPERT_GROUPS:
             nc.vector.tensor_copy(

@@ -23,8 +23,8 @@ HALF = T // 2
 QUARTER = T // 4
 
 WIDE_COLUMNS = 1376
-SCALAR_FROM = 3 * QUARTER
-GPSIMD_FROM = (None, 320, 288)
+SCALAR_FROM = 320
+GPSIMD_FROM = (None, 304, 288)
 WEIGHT_LOADS = ((0, 3), (3, 6), (6, 7), (7, 8))
 EXPERT_GROUPS = ((0, 3), (3, 6), (6, 8))
 VECTOR_BANKS_FROM = 6
@@ -104,6 +104,11 @@ def tile_routed_moe_kernel(tc, xT, w_words, w_scales, b, gate, offs, pos1, pos2,
                 in_=grouped[a][:, lo:hi, :].rearrange("p t j -> p (t j)"),
             )
 
+        def quantize_pass(a):
+            quantize(a, 3 * QUARTER, T)
+            quantize(a, 0, QUARTER)
+            quantize(a, QUARTER, 3 * QUARTER)
+
         def gather_words(a, lo, hi, width):
             nc.vector.tensor_copy(
                 out=slot_words[a][:, lo:hi],
@@ -128,25 +133,22 @@ def tile_routed_moe_kernel(tc, xT, w_words, w_scales, b, gate, offs, pos1, pos2,
             for e in range(lo, hi):
                 multiply(LAST, e)
                 cols = slice(e * C, (e + 1) * C)
-                if e < VECTOR_BANKS_FROM:
-                    nc.scalar.activation(out=y[:, cols], in_=acc[e][:], func=IDENTITY, bias=bias[:, e : e + 1])
-                else:
-                    nc.vector.tensor_scalar(out=y[:, cols], in0=acc[e][:], scalar1=bias[:, e : e + 1], scalar2=None, op0=ADD)
+                nc.scalar.activation(out=y[:, cols], in_=acc[e][:], func=IDENTITY, bias=bias[:, e : e + 1])
 
         round_pair(nc.vector.tensor_copy, 0, 0, 0, SCALAR_FROM)
         round_pair(nc.scalar.copy, 0, 0, SCALAR_FROM, T)
-        round_pair(nc.vector.tensor_copy, 0, 2, 0, HALF)
-        round_pair(nc.vector.tensor_copy, 0, 2, HALF, SCALAR_FROM)
+        round_pair(nc.vector.tensor_copy, 0, 2, 0, QUARTER)
+        round_pair(nc.vector.tensor_copy, 0, 2, QUARTER, SCALAR_FROM)
         round_pair(nc.scalar.copy, 0, 2, SCALAR_FROM, T)
-        quantize(0, 0, HALF)
-        quantize(0, HALF, T)
+        quantize(0, 0, QUARTER)
+        quantize(0, 3 * QUARTER, T)
+        quantize(0, QUARTER, 3 * QUARTER)
         gather_words(0, 0, ahead, pitch)
 
         round_pair(nc.scalar.copy, 1, 0, 0, GPSIMD_FROM[1])
         round_pair(nc.scalar.copy, 1, 2, 0, GPSIMD_FROM[1])
         round_on_gpsimd(1)
-        quantize(1, 0, HALF)
-        quantize(1, HALF, T)
+        quantize_pass(1)
         gather_words(0, ahead, SLOTS, reach)
         gather_words(1, 0, ahead, pitch)
 
@@ -155,8 +157,7 @@ def tile_routed_moe_kernel(tc, xT, w_words, w_scales, b, gate, offs, pos1, pos2,
             out=grouped[LAST][:, : GPSIMD_FROM[LAST], :].rearrange("p (c i) j -> p c j i", i=4),
             in_=raw[LAST][:, :, : GPSIMD_FROM[LAST]].rearrange("p j (c i) -> p c j i", i=4),
         )
-        quantize(LAST, 0, HALF)
-        quantize(LAST, HALF, T)
+        quantize_pass(LAST)
         gather_words(1, ahead, SLOTS, reach)
 
         for lo, hi in EXPERT_GROUPS:

@@ -145,9 +145,9 @@ def tile_routed_moe_kernel(tc, xT, w_words, w_scales, b, gate, offs, pos1, pos2,
         quantize(0, QUARTER, 3 * QUARTER)
         gather_words(0, 0, ahead, pitch)
 
-        round_pair(nc.scalar.copy, 1, 0, 0, GPSIMD_FROM[1])
-        round_pair(nc.scalar.copy, 1, 2, 0, GPSIMD_FROM[1])
-        round_on_gpsimd(1)
+        for first in (0, 2):
+            round_pair(nc.scalar.copy, 1, first, 0, HALF)
+            round_pair(nc.gpsimd.tensor_copy, 1, first, HALF, T)
         quantize_pass(1)
         gather_words(0, ahead, SLOTS, reach)
         gather_words(1, 0, ahead, pitch)

@@ -74,10 +74,10 @@ def tile_routed_moe_kernel(tc, xT, w_words, w_scales, b, gate, offs, pos1, pos2,
             nc.vector.memset(words[a][:, T:pitch], 0)
         nc.gpsimd.memset(wq_scales[:].bitcast(I32), 0)
 
-        for q in range(4):
+        for r in range(4):
             nc.sync.dma_start(
-                out=wq_scales[32 * q : 32 * q + 4, :].bitcast(I32).rearrange("r (g n) -> r g n", g=E * PASSES),
-                in_=w_scales[:, :, 4 * q : 4 * q + 4, :].bitcast(I32).rearrange("e a r n -> r (e a) n"),
+                out=wq_scales[r:P:32, :].bitcast(I32).rearrange("q (g n) -> q g n", g=E * PASSES),
+                in_=w_scales[:, :, r:16:4, :].bitcast(I32).rearrange("e a q n -> q (e a) n"),
             )
         nc.sync.dma_start(out=bias[:], in_=b)
         for lo, hi in WEIGHT_LOADS:

@@ -139,7 +139,8 @@ def tile_routed_moe_kernel(tc, xT, w_words, w_scales, b, gate, offs, pos1, pos2,
         round_pair(nc.scalar.copy, 0, 0, SCALAR_FROM, T)
         round_pair(nc.vector.tensor_copy, 0, 2, 0, QUARTER)
         round_pair(nc.vector.tensor_copy, 0, 2, QUARTER, SCALAR_FROM)
-        round_pair(nc.scalar.copy, 0, 2, SCALAR_FROM, T)
+        round_pair(nc.scalar.copy, 0, 2, 3 * QUARTER, T)
+        round_pair(nc.scalar.copy, 0, 2, SCALAR_FROM, 3 * QUARTER)
         quantize(0, 0, QUARTER)
         quantize(0, 3 * QUARTER, T)
         quantize(0, QUARTER, 3 * QUARTER)

@@ -25,7 +25,7 @@ QUARTER = T // 4
 WIDE_COLUMNS = 1376
 SCALAR_FROM = 320
 GPSIMD_FROM = (None, 304, 288)
-WEIGHT_LOADS = ((0, 3), (3, 6), (6, 7), (7, 8))
+WEIGHT_LOADS = ((0, 9), (9, 18), (18, 21), (21, 23), (23, 24))
 EXPERT_GROUPS = ((0, 3), (3, 6), (6, 8))
 VECTOR_BANKS_FROM = 6
 
@@ -82,8 +82,8 @@ def tile_routed_moe_kernel(tc, xT, w_words, w_scales, b, gate, offs, pos1, pos2,
         nc.sync.dma_start(out=bias[:], in_=b)
         for lo, hi in WEIGHT_LOADS:
             nc.sync.dma_start(
-                out=wq[:, lo * PASSES * N : hi * PASSES * N].bitcast(I32).rearrange("p (g n) -> p g n", n=N),
-                in_=w_words[lo:hi].rearrange("e a p n r -> p (e a) (n r)").bitcast(I32),
+                out=wq[:, lo * N : hi * N].bitcast(I32).rearrange("p (g n) -> p g n", n=N),
+                in_=w_words.rearrange("e a p n r -> p (e a) (n r)")[:, lo:hi, :].bitcast(I32),
             )
         nc.sync.dma_start(pos1_sb[:], pos1)
         nc.sync.dma_start(pos2_sb[:], pos2)
@@ -189,8 +189,6 @@ def tile_routed_moe_kernel(tc, xT, w_words, w_scales, b, gate, offs, pos1, pos2,
 
         nc.vector.tensor_tensor(out=part1[:], in0=y[:].indirect(pos1_sb[:]), in1=gates[:, 0, :], op=MULT)
         second_product(0, HALF)
-        second_product(HALF, HALF + QUARTER)
-        add_and_store(0, HALF)
-        second_product(HALF + QUARTER, T)
-        add_and_store(HALF, HALF + QUARTER)
-        add_and_store(HALF + QUARTER, T)
+        second_product(HALF, T)
+        for lo in range(0, T, QUARTER):
+            add_and_store(lo, lo + QUARTER)

@@ -12,6 +12,7 @@ FP8X4 = mybir.dt.float8_e4m3fn_x4
 MULT = mybir.AluOpType.mult
 ADD = mybir.AluOpType.add
 IDENTITY = mybir.ActivationFunctionType.Identity
+COPY = mybir.ActivationFunctionType.Copy
 
 P = 128
 K, T, E, C, N = 1536, 512, 8, 128, 128
@@ -22,12 +23,13 @@ FLOPS = 2 * K * N * SLOTS
 HALF = T // 2
 QUARTER = T // 4
 
-WIDE_COLUMNS = 1376
+PITCH = 1152
+EARLY = 864
+REACH = PITCH + QUARTER
 SCALAR_FROM = 320
-GPSIMD_FROM = (None, 304, 288)
+GPSIMD_FROM = 288
 WEIGHT_LOADS = ((0, 9), (9, 18), (18, 21), (21, 23), (23, 24))
 EXPERT_GROUPS = ((0, 3), (3, 6), (6, 8))
-VECTOR_BANKS_FROM = 6
 
 
 def tile_routed_moe_kernel(tc, xT, w_words, w_scales, b, gate, offs, pos1, pos2, out):
@@ -42,9 +44,8 @@ def tile_routed_moe_kernel(tc, xT, w_words, w_scales, b, gate, offs, pos1, pos2,
 
         raw = [keep.tile([P, 4, T], F32, name=f"raw{a}") for a in range(PASSES)]
         grouped = [keep.tile([P, T, 4], BF16, name=f"grouped{a}", align_bytes=64) for a in range(PASSES)]
-        pitch, reach, ahead = 1152, 1280, 864
-        all_words = keep.tile([P, LAST * pitch + T], I32, name="all_words", align_bytes=64)
-        words = [all_words[:, a * pitch :] for a in range(PASSES)]
+        all_words = keep.tile([P, LAST * PITCH + T], I32, name="all_words", align_bytes=64)
+        words = [all_words[:, a * PITCH :] for a in range(PASSES)]
         scales = keep.tile([P, T], U8, name="scales", align_bytes=64)
         slot_words = [keep.tile([P, SLOTS], U32, name=f"slot_words{a}", align_bytes=64) for a in range(PASSES)]
         slot_scales = keep.tile([P, SLOTS], U8, name="slot_scales", align_bytes=64)
@@ -53,6 +54,7 @@ def tile_routed_moe_kernel(tc, xT, w_words, w_scales, b, gate, offs, pos1, pos2,
         bias = keep.tile([P, E], F32, name="bias")
         gates = keep.tile([P, 2, T], F32, name="gates")
         y = keep.tile([P, SLOTS], F32, name="y")
+        second = keep.tile([P, T], F32, name="second")
         part1 = keep.tile([P, T], F32, name="part1")
         part2 = keep.tile([P, T], F32, name="part2")
         total = keep.tile([P, T], F32, name="total")
@@ -71,7 +73,7 @@ def tile_routed_moe_kernel(tc, xT, w_words, w_scales, b, gate, offs, pos1, pos2,
 
         nc.vector.memset(scales[:].bitcast(I32), 0)
         for a in range(LAST):
-            nc.vector.memset(words[a][:, T:pitch], 0)
+            nc.vector.memset(words[a][:, T:PITCH], 0)
         nc.gpsimd.memset(wq_scales[:].bitcast(I32), 0)
 
         for r in range(4):
@@ -92,10 +94,6 @@ def tile_routed_moe_kernel(tc, xT, w_words, w_scales, b, gate, offs, pos1, pos2,
 
         def round_pair(copy, a, first, lo, hi):
             copy(out=grouped[a][:, lo:hi, first : first + 2], in_=raw[a][:, first : first + 2, lo:hi].rearrange("p j t -> p t j"))
-
-        def round_on_gpsimd(a):
-            lo = GPSIMD_FROM[a]
-            nc.gpsimd.tensor_copy(out=grouped[a][:, lo:, :], in_=raw[a][:, :, lo:].rearrange("p j t -> p t j"))
 
         def quantize(a, lo, hi):
             nc.vector.quantize_mx(
@@ -144,22 +142,22 @@ def tile_routed_moe_kernel(tc, xT, w_words, w_scales, b, gate, offs, pos1, pos2,
         quantize(0, 0, QUARTER)
         quantize(0, 3 * QUARTER, T)
         quantize(0, QUARTER, 3 * QUARTER)
-        gather_words(0, 0, ahead, pitch)
+        gather_words(0, 0, EARLY, PITCH)
 
         for first in (0, 2):
             round_pair(nc.scalar.copy, 1, first, 0, HALF)
             round_pair(nc.gpsimd.tensor_copy, 1, first, HALF, T)
         quantize_pass(1)
-        gather_words(0, ahead, SLOTS, reach)
-        gather_words(1, 0, ahead, pitch)
+        gather_words(0, EARLY, SLOTS, REACH)
+        gather_words(1, 0, EARLY, PITCH)
 
-        round_on_gpsimd(LAST)
+        nc.gpsimd.tensor_copy(out=grouped[LAST][:, GPSIMD_FROM:, :], in_=raw[LAST][:, :, GPSIMD_FROM:].rearrange("p j t -> p t j"))
         nc.scalar.copy(
-            out=grouped[LAST][:, : GPSIMD_FROM[LAST], :].rearrange("p (c i) j -> p c j i", i=4),
-            in_=raw[LAST][:, :, : GPSIMD_FROM[LAST]].rearrange("p j (c i) -> p c j i", i=4),
+            out=grouped[LAST][:, :GPSIMD_FROM, :].rearrange("p (c i) j -> p c j i", i=4),
+            in_=raw[LAST][:, :, :GPSIMD_FROM].rearrange("p j (c i) -> p c j i", i=4),
         )
         quantize_pass(LAST)
-        gather_words(1, ahead, SLOTS, reach)
+        gather_words(1, EARLY, SLOTS, REACH)
 
         for lo, hi in EXPERT_GROUPS:
             nc.vector.tensor_copy(
@@ -175,20 +173,13 @@ def tile_routed_moe_kernel(tc, xT, w_words, w_scales, b, gate, offs, pos1, pos2,
                 for e in range(lo, hi):
                     finish(e, e + 1)
 
-        def second_product(lo, hi):
-            nc.vector.tensor_tensor(
-                out=part2[:, lo:hi],
-                in0=y[:].indirect(pos2_sb[:, lo // 16 : hi // 16]),
-                in1=gates[:, 1, lo:hi],
-                op=MULT,
-            )
-
-        def add_and_store(lo, hi):
-            nc.vector.tensor_tensor(out=total[:, lo:hi], in0=part1[:, lo:hi], in1=part2[:, lo:hi], op=ADD)
-            nc.sync.dma_start(out=out[:, lo:hi], in_=total[:, lo:hi])
-
+        halves = [slice(lo, lo + HALF) for lo in range(0, T, HALF)]
         nc.vector.tensor_tensor(out=part1[:], in0=y[:].indirect(pos1_sb[:]), in1=gates[:, 0, :], op=MULT)
-        second_product(0, HALF)
-        second_product(HALF, T)
+        for half in halves:
+            nc.scalar.activation(out=second[:, half], in_=y[:].indirect(pos2_sb[:, half.start // 16 : half.stop // 16]), func=COPY)
+        for half in halves:
+            nc.vector.tensor_tensor(out=part2[:, half], in0=second[:, half], in1=gates[:, 1, half], op=MULT)
         for lo in range(0, T, QUARTER):
-            add_and_store(lo, lo + QUARTER)
+            cols = slice(lo, lo + QUARTER)
+            nc.vector.tensor_tensor(out=total[:, cols], in0=part1[:, cols], in1=part2[:, cols], op=ADD)
+            nc.sync.dma_start(out=out[:, cols], in_=total[:, cols])

@@ -28,7 +28,7 @@ EARLY = 864
 REACH = PITCH + QUARTER
 SCALAR_FROM = 320
 GPSIMD_FROM = 288
-WEIGHT_LOADS = ((0, 9), (9, 18), (18, 21), (21, 23), (23, 24))
+WEIGHT_LOADS = ((0, 3), (3, 9), (9, 15), (15, 18), (18, 21), (21, 24))
 EXPERT_GROUPS = ((0, 3), (3, 6), (6, 8))
 
 
@@ -81,12 +81,17 @@ def tile_routed_moe_kernel(tc, xT, w_words, w_scales, b, gate, offs, pos1, pos2,
                 out=wq_scales[r:P:32, :].bitcast(I32).rearrange("q (g n) -> q g n", g=E * PASSES),
                 in_=w_scales[:, :, r:16:4, :].bitcast(I32).rearrange("e a q n -> q (e a) n"),
             )
-        nc.sync.dma_start(out=bias[:], in_=b)
-        for lo, hi in WEIGHT_LOADS:
+
+        def load_weights(lo, hi):
             nc.sync.dma_start(
                 out=wq[:, lo * N : hi * N].bitcast(I32).rearrange("p (g n) -> p g n", n=N),
                 in_=w_words.rearrange("e a p n r -> p (e a) (n r)")[:, lo:hi, :].bitcast(I32),
             )
+
+        load_weights(*WEIGHT_LOADS[0])
+        nc.sync.dma_start(out=bias[:], in_=b)
+        for lo, hi in WEIGHT_LOADS[1:]:
+            load_weights(lo, hi)
         nc.sync.dma_start(pos1_sb[:], pos1)
         nc.sync.dma_start(pos2_sb[:], pos2)
         for g in range(2):
@@ -179,7 +184,7 @@ def tile_routed_moe_kernel(tc, xT, w_words, w_scales, b, gate, offs, pos1, pos2,
             nc.scalar.activation(out=second[:, half], in_=y[:].indirect(pos2_sb[:, half.start // 16 : half.stop // 16]), func=COPY)
         for half in halves:
             nc.vector.tensor_tensor(out=part2[:, half], in0=second[:, half], in1=gates[:, 1, half], op=MULT)
-        for lo in range(0, T, QUARTER):
-            cols = slice(lo, lo + QUARTER)
+        for lo, hi in ((0, HALF), (HALF, 3 * QUARTER), (3 * QUARTER, T)):
+            cols = slice(lo, hi)
             nc.vector.tensor_tensor(out=total[:, cols], in0=part1[:, cols], in1=part2[:, cols], op=ADD)
             nc.sync.dma_start(out=out[:, cols], in_=total[:, cols])

@@ -178,13 +178,22 @@ def tile_routed_moe_kernel(tc, xT, w_words, w_scales, b, gate, offs, pos1, pos2,
                 for e in range(lo, hi):
                     finish(e, e + 1)
 
-        halves = [slice(lo, lo + HALF) for lo in range(0, T, HALF)]
-        nc.vector.tensor_tensor(out=part1[:], in0=y[:].indirect(pos1_sb[:]), in1=gates[:, 0, :], op=MULT)
-        for half in halves:
-            nc.scalar.activation(out=second[:, half], in_=y[:].indirect(pos2_sb[:, half.start // 16 : half.stop // 16]), func=COPY)
-        for half in halves:
-            nc.vector.tensor_tensor(out=part2[:, half], in0=second[:, half], in1=gates[:, 1, half], op=MULT)
-        for lo, hi in ((0, HALF), (HALF, 3 * QUARTER), (3 * QUARTER, T)):
-            cols = slice(lo, hi)
-            nc.vector.tensor_tensor(out=total[:, cols], in0=part1[:, cols], in1=part2[:, cols], op=ADD)
-            nc.sync.dma_start(out=out[:, cols], in_=total[:, cols])
+        def first_product(lo, hi):
+            nc.vector.tensor_tensor(out=part1[:, lo:hi], in0=y[:].indirect(pos1_sb[:, lo // 16 : hi // 16]), in1=gates[:, 0, lo:hi], op=MULT)
+
+        def second_product(lo, hi):
+            nc.scalar.activation(out=second[:, lo:hi], in_=y[:].indirect(pos2_sb[:, lo // 16 : hi // 16]), func=COPY)
+            nc.vector.tensor_tensor(out=part2[:, lo:hi], in0=second[:, lo:hi], in1=gates[:, 1, lo:hi], op=MULT)
+
+        def add_and_store(lo, hi):
+            nc.vector.tensor_tensor(out=total[:, lo:hi], in0=part1[:, lo:hi], in1=part2[:, lo:hi], op=ADD)
+            nc.sync.dma_start(out=out[:, lo:hi], in_=total[:, lo:hi])
+
+        first_product(0, 3 * QUARTER)
+        second_product(0, HALF)
+        first_product(3 * QUARTER, T)
+        add_and_store(0, HALF)
+        second_product(HALF, 3 * QUARTER)
+        second_product(3 * QUARTER, T)
+        add_and_store(HALF, 3 * QUARTER)
+        add_and_store(3 * QUARTER, T)

@@ -30,6 +30,7 @@ SCALAR_FROM = 320
 GPSIMD_FROM = 288
 WEIGHT_LOADS = ((0, 3), (3, 9), (9, 15), (15, 18), (18, 21), (21, 24))
 EXPERT_GROUPS = ((0, 3), (3, 6), (6, 8))
+LAST_CUT = 448
 
 
 def tile_routed_moe_kernel(tc, xT, w_words, w_scales, b, gate, offs, pos1, pos2, out):
@@ -178,9 +179,6 @@ def tile_routed_moe_kernel(tc, xT, w_words, w_scales, b, gate, offs, pos1, pos2,
                 for e in range(lo, hi):
                     finish(e, e + 1)
 
-        def first_product(lo, hi):
-            nc.vector.tensor_tensor(out=part1[:, lo:hi], in0=y[:].indirect(pos1_sb[:, lo // 16 : hi // 16]), in1=gates[:, 0, lo:hi], op=MULT)
-
         def second_product(lo, hi):
             nc.scalar.activation(out=second[:, lo:hi], in_=y[:].indirect(pos2_sb[:, lo // 16 : hi // 16]), func=COPY)
             nc.vector.tensor_tensor(out=part2[:, lo:hi], in0=second[:, lo:hi], in1=gates[:, 1, lo:hi], op=MULT)
@@ -189,11 +187,8 @@ def tile_routed_moe_kernel(tc, xT, w_words, w_scales, b, gate, offs, pos1, pos2,
             nc.vector.tensor_tensor(out=total[:, lo:hi], in0=part1[:, lo:hi], in1=part2[:, lo:hi], op=ADD)
             nc.sync.dma_start(out=out[:, lo:hi], in_=total[:, lo:hi])
 
-        first_product(0, 3 * QUARTER)
-        second_product(0, HALF)
-        first_product(3 * QUARTER, T)
-        add_and_store(0, HALF)
-        second_product(HALF, 3 * QUARTER)
-        second_product(3 * QUARTER, T)
-        add_and_store(HALF, 3 * QUARTER)
-        add_and_store(3 * QUARTER, T)
+        nc.vector.tensor_tensor(out=part1[:], in0=y[:].indirect(pos1_sb[:]), in1=gates[:, 0, :], op=MULT)
+        for lo, hi in ((0, HALF), (HALF, LAST_CUT), (LAST_CUT, T)):
+            second_product(lo, hi)
+        for lo, hi in ((0, HALF), (HALF, 3 * QUARTER), (3 * QUARTER, T)):
+            add_and_store(lo, hi)

@@ -31,6 +31,7 @@ GPSIMD_FROM = 288
 WEIGHT_LOADS = ((0, 3), (3, 9), (9, 15), (15, 18), (18, 21), (21, 24))
 EXPERT_GROUPS = ((0, 3), (3, 6), (6, 8))
 LAST_CUT = 448
+FIRST_STORE = 192
 
 
 def tile_routed_moe_kernel(tc, xT, w_words, w_scales, b, gate, offs, pos1, pos2, out):
@@ -190,5 +191,5 @@ def tile_routed_moe_kernel(tc, xT, w_words, w_scales, b, gate, offs, pos1, pos2,
         nc.vector.tensor_tensor(out=part1[:], in0=y[:].indirect(pos1_sb[:]), in1=gates[:, 0, :], op=MULT)
         for lo, hi in ((0, HALF), (HALF, LAST_CUT), (LAST_CUT, T)):
             second_product(lo, hi)
-        for lo, hi in ((0, HALF), (HALF, 3 * QUARTER), (3 * QUARTER, T)):
+        for lo, hi in ((0, FIRST_STORE), (FIRST_STORE, 3 * QUARTER), (3 * QUARTER, T)):
             add_and_store(lo, hi)

@@ -28,7 +28,7 @@ EARLY = 864
 REACH = PITCH + QUARTER
 SCALAR_FROM = 320
 GPSIMD_FROM = 288
-WEIGHT_LOADS = ((0, 3), (3, 9), (9, 15), (15, 18), (18, 21), (21, 24))
+WEIGHT_LOADS = ((0, 3), (3, 9), (9, 18), (18, 21), (21, 24))
 EXPERT_GROUPS = ((0, 3), (3, 6), (6, 8))
 LAST_CUT = 448
 FIRST_STORE = 192
@@ -71,7 +71,8 @@ def tile_routed_moe_kernel(tc, xT, w_words, w_scales, b, gate, offs, pos1, pos2,
         nc.sync.dma_start(offs_sb[:], offs)
         load_x(1, 0, 2)
         load_x(1, 2, 2)
-        load_x(2, 0, 4)
+        load_x(2, 0, 2)
+        load_x(2, 2, 2)
 
         nc.vector.memset(scales[:].bitcast(I32), 0)
         for a in range(LAST):
@@ -158,11 +159,12 @@ def tile_routed_moe_kernel(tc, xT, w_words, w_scales, b, gate, offs, pos1, pos2,
         gather_words(0, EARLY, SLOTS, REACH)
         gather_words(1, 0, EARLY, PITCH)
 
-        nc.gpsimd.tensor_copy(out=grouped[LAST][:, GPSIMD_FROM:, :], in_=raw[LAST][:, :, GPSIMD_FROM:].rearrange("p j t -> p t j"))
-        nc.scalar.copy(
-            out=grouped[LAST][:, :GPSIMD_FROM, :].rearrange("p (c i) j -> p c j i", i=4),
-            in_=raw[LAST][:, :, :GPSIMD_FROM].rearrange("p j (c i) -> p c j i", i=4),
-        )
+        blocks_out = grouped[LAST][:, : 3 * QUARTER, :].rearrange("p (c t) j -> p c t j", t=64)
+        blocks_in = raw[LAST][:, :, : 3 * QUARTER].rearrange("p j (c t) -> p c t j", t=64)
+        for first in (0, 2):
+            round_pair(nc.scalar.copy, LAST, first, 3 * QUARTER, T)
+            nc.scalar.copy(out=blocks_out[:, :, :32, first : first + 2], in_=blocks_in[:, :, :32, first : first + 2])
+        nc.gpsimd.tensor_copy(out=blocks_out[:, :, 32:, :], in_=blocks_in[:, :, 32:, :])
         quantize_pass(LAST)
         gather_words(1, EARLY, SLOTS, REACH)
 

@@ -26,8 +26,8 @@ QUARTER = T // 4
 PITCH = 1152
 EARLY = 864
 REACH = PITCH + QUARTER
-SCALAR_FROM = 320
-GPSIMD_FROM = 288
+SCALAR_FROM = 288
+GPSIMD_TO = 208
 WEIGHT_LOADS = ((0, 3), (3, 9), (9, 18), (18, 21), (21, 24))
 EXPERT_GROUPS = ((0, 3), (3, 6), (6, 8))
 LAST_CUT = 448
@@ -147,14 +147,15 @@ def tile_routed_moe_kernel(tc, xT, w_words, w_scales, b, gate, offs, pos1, pos2,
         round_pair(nc.vector.tensor_copy, 0, 2, QUARTER, SCALAR_FROM)
         round_pair(nc.scalar.copy, 0, 2, 3 * QUARTER, T)
         round_pair(nc.scalar.copy, 0, 2, SCALAR_FROM, 3 * QUARTER)
-        quantize(0, 0, QUARTER)
-        quantize(0, 3 * QUARTER, T)
-        quantize(0, QUARTER, 3 * QUARTER)
+        for quarter in (0, 3, 1, 2):
+            quantize(0, quarter * QUARTER, (quarter + 1) * QUARTER)
         gather_words(0, 0, EARLY, PITCH)
 
+        round_pair(nc.scalar.copy, 1, 0, GPSIMD_TO, T)
+        round_pair(nc.scalar.copy, 1, 2, 3 * QUARTER, T)
+        round_pair(nc.scalar.copy, 1, 2, GPSIMD_TO, 3 * QUARTER)
         for first in (0, 2):
-            round_pair(nc.scalar.copy, 1, first, 0, HALF)
-            round_pair(nc.gpsimd.tensor_copy, 1, first, HALF, T)
+            round_pair(nc.gpsimd.tensor_copy, 1, first, 0, GPSIMD_TO)
         quantize_pass(1)
         gather_words(0, EARLY, SLOTS, REACH)
         gather_words(1, 0, EARLY, PITCH)

@@ -111,9 +111,8 @@ def tile_routed_moe_kernel(tc, xT, w_words, w_scales, b, gate, offs, pos1, pos2,
             )
 
         def quantize_pass(a):
-            quantize(a, 3 * QUARTER, T)
-            quantize(a, 0, QUARTER)
-            quantize(a, QUARTER, 3 * QUARTER)
+            quantize(a, 0, HALF)
+            quantize(a, HALF, T)
 
         def gather_words(a, lo, hi, width):
             nc.vector.tensor_copy(
@@ -152,8 +151,8 @@ def tile_routed_moe_kernel(tc, xT, w_words, w_scales, b, gate, offs, pos1, pos2,
         gather_words(0, 0, EARLY, PITCH)
 
         round_pair(nc.scalar.copy, 1, 0, GPSIMD_TO, T)
-        round_pair(nc.scalar.copy, 1, 2, 3 * QUARTER, T)
-        round_pair(nc.scalar.copy, 1, 2, GPSIMD_TO, 3 * QUARTER)
+        round_pair(nc.scalar.copy, 1, 2, GPSIMD_TO, HALF)
+        round_pair(nc.scalar.copy, 1, 2, HALF, T)
         for first in (0, 2):
             round_pair(nc.gpsimd.tensor_copy, 1, first, 0, GPSIMD_TO)
         quantize_pass(1)

@@ -28,8 +28,9 @@ EARLY = 864
 REACH = PITCH + QUARTER
 SCALAR_FROM = 288
 GPSIMD_TO = 208
-WEIGHT_LOADS = ((0, 3), (3, 9), (9, 18), (18, 21), (21, 24))
-EXPERT_GROUPS = ((0, 3), (3, 6), (6, 8))
+WEIGHT_LOADS = ((0, 2), (2, 11), (11, 17), (17, 23), (23, 24))
+EXPERT_GROUPS = ((0, 4), (4, 8))
+WIDE = T + HALF
 LAST_CUT = 448
 FIRST_STORE = 192
 
@@ -46,9 +47,9 @@ def tile_routed_moe_kernel(tc, xT, w_words, w_scales, b, gate, offs, pos1, pos2,
 
         raw = [keep.tile([P, 4, T], F32, name=f"raw{a}") for a in range(PASSES)]
         grouped = [keep.tile([P, T, 4], BF16, name=f"grouped{a}", align_bytes=64) for a in range(PASSES)]
-        all_words = keep.tile([P, LAST * PITCH + T], I32, name="all_words", align_bytes=64)
+        all_words = keep.tile([P, LAST * PITCH + WIDE], I32, name="all_words", align_bytes=64)
         words = [all_words[:, a * PITCH :] for a in range(PASSES)]
-        scales = keep.tile([P, T], U8, name="scales", align_bytes=64)
+        scales = keep.tile([P, WIDE], U8, name="scales", align_bytes=64)
         slot_words = [keep.tile([P, SLOTS], U32, name=f"slot_words{a}", align_bytes=64) for a in range(PASSES)]
         slot_scales = keep.tile([P, SLOTS], U8, name="slot_scales", align_bytes=64)
         wq = keep.tile([P, E * PASSES * N], U32, name="wq", align_bytes=64)
@@ -77,6 +78,7 @@ def tile_routed_moe_kernel(tc, xT, w_words, w_scales, b, gate, offs, pos1, pos2,
         nc.vector.memset(scales[:].bitcast(I32), 0)
         for a in range(LAST):
             nc.vector.memset(words[a][:, T:PITCH], 0)
+        nc.vector.memset(words[LAST][:, T:WIDE], 0)
         nc.gpsimd.memset(wq_scales[:].bitcast(I32), 0)
 
         for r in range(4):
@@ -134,7 +136,7 @@ def tile_routed_moe_kernel(tc, xT, w_words, w_scales, b, gate, offs, pos1, pos2,
             )
 
         def finish(lo, hi):
-            gather_words(LAST, lo * C, hi * C, T)
+            gather_words(LAST, lo * C, hi * C, WIDE)
             for e in range(lo, hi):
                 multiply(LAST, e)
                 cols = slice(e * C, (e + 1) * C)
@@ -179,8 +181,9 @@ def tile_routed_moe_kernel(tc, xT, w_words, w_scales, b, gate, offs, pos1, pos2,
             if hi < E:
                 finish(lo, hi)
             else:
-                for e in range(lo, hi):
-                    finish(e, e + 1)
+                finish(lo, E - 2)
+                finish(E - 2, E - 1)
+                finish(E - 1, E)
 
         def second_product(lo, hi):
             nc.scalar.activation(out=second[:, lo:hi], in_=y[:].indirect(pos2_sb[:, lo // 16 : hi // 16]), func=COPY)

@@ -28,8 +28,8 @@ EARLY = 864
 REACH = PITCH + QUARTER
 SCALAR_FROM = 288
 GPSIMD_TO = 208
-WEIGHT_LOADS = ((0, 2), (2, 11), (11, 17), (17, 23), (23, 24))
-EXPERT_GROUPS = ((0, 4), (4, 8))
+HALVES = ((0, E // 2), (E // 2, E))
+LAST_GROUPS = ((0, 3), (3, 5), (5, 7), (7, 8))
 WIDE = T + HALF
 LAST_CUT = 448
 FIRST_STORE = 192
@@ -47,7 +47,7 @@ def tile_routed_moe_kernel(tc, xT, w_words, w_scales, b, gate, offs, pos1, pos2,
 
         raw = [keep.tile([P, 4, T], F32, name=f"raw{a}") for a in range(PASSES)]
         grouped = [keep.tile([P, T, 4], BF16, name=f"grouped{a}", align_bytes=64) for a in range(PASSES)]
-        all_words = keep.tile([P, LAST * PITCH + WIDE], I32, name="all_words", align_bytes=64)
+        all_words = keep.tile([P, LAST * PITCH + T], I32, name="all_words", align_bytes=64)
         words = [all_words[:, a * PITCH :] for a in range(PASSES)]
         scales = keep.tile([P, WIDE], U8, name="scales", align_bytes=64)
         slot_words = [keep.tile([P, SLOTS], U32, name=f"slot_words{a}", align_bytes=64) for a in range(PASSES)]
@@ -78,7 +78,6 @@ def tile_routed_moe_kernel(tc, xT, w_words, w_scales, b, gate, offs, pos1, pos2,
         nc.vector.memset(scales[:].bitcast(I32), 0)
         for a in range(LAST):
             nc.vector.memset(words[a][:, T:PITCH], 0)
-        nc.vector.memset(words[LAST][:, T:WIDE], 0)
         nc.gpsimd.memset(wq_scales[:].bitcast(I32), 0)
 
         for r in range(4):
@@ -87,20 +86,21 @@ def tile_routed_moe_kernel(tc, xT, w_words, w_scales, b, gate, offs, pos1, pos2,
                 in_=w_scales[:, :, r:16:4, :].bitcast(I32).rearrange("e a q n -> q (e a) n"),
             )
 
-        def load_weights(lo, hi):
+        def load_weights(a, lo, hi):
             nc.sync.dma_start(
-                out=wq[:, lo * N : hi * N].bitcast(I32).rearrange("p (g n) -> p g n", n=N),
-                in_=w_words.rearrange("e a p n r -> p (e a) (n r)")[:, lo:hi, :].bitcast(I32),
+                out=wq[:].bitcast(I32).rearrange("p (e a n) -> p e a n", a=PASSES, n=N)[:, lo:hi, a, :],
+                in_=w_words.rearrange("e a p n r -> p e a (n r)")[:, lo:hi, a, :].bitcast(I32),
             )
 
-        load_weights(*WEIGHT_LOADS[0])
+        for lo, hi in HALVES:
+            for a in range(LAST):
+                load_weights(a, lo, hi)
         nc.sync.dma_start(out=bias[:], in_=b)
-        for lo, hi in WEIGHT_LOADS[1:]:
-            load_weights(lo, hi)
+        for lo, hi in HALVES:
+            load_weights(LAST, lo, hi)
         nc.sync.dma_start(pos1_sb[:], pos1)
         nc.sync.dma_start(pos2_sb[:], pos2)
-        for g in range(2):
-            nc.sync.dma_start(out=gates[:, g, :], in_=gate[g])
+        nc.sync.dma_start(out=gates[:], in_=gate.rearrange("g n t -> n g t"))
 
         def round_pair(copy, a, first, lo, hi):
             copy(out=grouped[a][:, lo:hi, first : first + 2], in_=raw[a][:, first : first + 2, lo:hi].rearrange("p j t -> p t j"))
@@ -136,7 +136,7 @@ def tile_routed_moe_kernel(tc, xT, w_words, w_scales, b, gate, offs, pos1, pos2,
             )
 
         def finish(lo, hi):
-            gather_words(LAST, lo * C, hi * C, WIDE)
+            gather_words(LAST, lo * C, hi * C, T)
             for e in range(lo, hi):
                 multiply(LAST, e)
                 cols = slice(e * C, (e + 1) * C)
@@ -170,20 +170,16 @@ def tile_routed_moe_kernel(tc, xT, w_words, w_scales, b, gate, offs, pos1, pos2,
         quantize_pass(LAST)
         gather_words(1, EARLY, SLOTS, REACH)
 
-        for lo, hi in EXPERT_GROUPS:
+        for lo, hi in HALVES:
             nc.vector.tensor_copy(
                 out=slot_scales[:, lo * C : hi * C],
                 in_=scales[:].indirect(offs_sb[:, lo * C // 16 : hi * C // 16]),
             )
-            for e in range(lo, hi):
-                for a in range(LAST):
+            for a in range(LAST):
+                for e in range(lo, hi):
                     multiply(a, e)
-            if hi < E:
-                finish(lo, hi)
-            else:
-                finish(lo, E - 2)
-                finish(E - 2, E - 1)
-                finish(E - 1, E)
+        for lo, hi in LAST_GROUPS:
+            finish(lo, hi)
 
         def second_product(lo, hi):
             nc.scalar.activation(out=second[:, lo:hi], in_=y[:].indirect(pos2_sb[:, lo // 16 : hi // 16]), func=COPY)

@@ -28,6 +28,7 @@ EARLY = 864
 REACH = PITCH + QUARTER
 SCALAR_FROM = 288
 GPSIMD_TO = 208
+GPSIMD_WHOLE = 224
 HALVES = ((0, E // 2), (E // 2, E))
 LAST_GROUPS = ((0, 3), (3, 5), (5, 7), (7, 8))
 WIDE = T + HALF
@@ -72,8 +73,7 @@ def tile_routed_moe_kernel(tc, xT, w_words, w_scales, b, gate, offs, pos1, pos2,
         nc.sync.dma_start(offs_sb[:], offs)
         load_x(1, 0, 2)
         load_x(1, 2, 2)
-        load_x(2, 0, 2)
-        load_x(2, 2, 2)
+        load_x(2, 0, 4)
 
         nc.vector.memset(scales[:].bitcast(I32), 0)
         for a in range(LAST):
@@ -100,7 +100,8 @@ def tile_routed_moe_kernel(tc, xT, w_words, w_scales, b, gate, offs, pos1, pos2,
             load_weights(LAST, lo, hi)
         nc.sync.dma_start(pos1_sb[:], pos1)
         nc.sync.dma_start(pos2_sb[:], pos2)
-        nc.sync.dma_start(out=gates[:], in_=gate.rearrange("g n t -> n g t"))
+        for g in range(2):
+            nc.sync.dma_start(out=gates[:, g, :], in_=gate[g])
 
         def round_pair(copy, a, first, lo, hi):
             copy(out=grouped[a][:, lo:hi, first : first + 2], in_=raw[a][:, first : first + 2, lo:hi].rearrange("p j t -> p t j"))
@@ -161,12 +162,10 @@ def tile_routed_moe_kernel(tc, xT, w_words, w_scales, b, gate, offs, pos1, pos2,
         gather_words(0, EARLY, SLOTS, REACH)
         gather_words(1, 0, EARLY, PITCH)
 
-        blocks_out = grouped[LAST][:, : 3 * QUARTER, :].rearrange("p (c t) j -> p c t j", t=64)
-        blocks_in = raw[LAST][:, :, : 3 * QUARTER].rearrange("p j (c t) -> p c t j", t=64)
-        for first in (0, 2):
-            round_pair(nc.scalar.copy, LAST, first, 3 * QUARTER, T)
-            nc.scalar.copy(out=blocks_out[:, :, :32, first : first + 2], in_=blocks_in[:, :, :32, first : first + 2])
-        nc.gpsimd.tensor_copy(out=blocks_out[:, :, 32:, :], in_=blocks_in[:, :, 32:, :])
+        whole_in = raw[LAST][:].rearrange("p j t -> p t j")
+        nc.gpsimd.tensor_copy(out=grouped[LAST][:, :GPSIMD_WHOLE, :], in_=whole_in[:, :GPSIMD_WHOLE, :])
+        nc.scalar.copy(out=grouped[LAST][:, GPSIMD_WHOLE:HALF, :], in_=whole_in[:, GPSIMD_WHOLE:HALF, :])
+        nc.scalar.copy(out=grouped[LAST][:, HALF:, :], in_=whole_in[:, HALF:, :])
         quantize_pass(LAST)
         gather_words(1, EARLY, SLOTS, REACH)
 

from contextlib import ExitStack

import concourse.mybir as mybir

F32 = mybir.dt.float32
BF16 = mybir.dt.bfloat16
I32 = mybir.dt.int32
U32 = mybir.dt.uint32
U16 = mybir.dt.uint16
U8 = mybir.dt.uint8
FP8X4 = mybir.dt.float8_e4m3fn_x4
MULT = mybir.AluOpType.mult
ADD = mybir.AluOpType.add
IDENTITY = mybir.ActivationFunctionType.Identity
COPY = mybir.ActivationFunctionType.Copy

P = 128
K, T, E, C, N = 1536, 512, 8, 128, 128
SLOTS = E * C
PASSES = K // 512
LAST = PASSES - 1
FLOPS = 2 * K * N * SLOTS
HALF = T // 2
QUARTER = T // 4

PITCH = 1152
EARLY = 864
REACH = PITCH + QUARTER
SCALAR_FROM = 288
GPSIMD_TO = 208
GPSIMD_WHOLE = 224
HALVES = ((0, E // 2), (E // 2, E))
LAST_GROUPS = ((0, 3), (3, 5), (5, 7), (7, 8))
WIDE = T + HALF
LAST_CUT = 448
FIRST_STORE = 192


def tile_routed_moe_kernel(tc, xT, w_words, w_scales, b, gate, offs, pos1, pos2, out):
    nc = tc.nc
    with ExitStack() as ctx:
        keep = ctx.enter_context(tc.tile_pool(name="keep", bufs=1))
        psum = ctx.enter_context(tc.psum_pool(name="psum", bufs=1))

        offs_sb = keep.tile([P, SLOTS // 16], U16, name="offs_sb")
        pos1_sb = keep.tile([P, T // 16], U16, name="pos1_sb")
        pos2_sb = keep.tile([P, T // 16], U16, name="pos2_sb")

        raw = [keep.tile([P, 4, T], F32, name=f"raw{a}") for a in range(PASSES)]
        grouped = [keep.tile([P, T, 4], BF16, name=f"grouped{a}", align_bytes=64) for a in range(PASSES)]
        all_words = keep.tile([P, LAST * PITCH + T], I32, name="all_words", align_bytes=64)
        words = [all_words[:, a * PITCH :] for a in range(PASSES)]
        scales = keep.tile([P, WIDE], U8, name="scales", align_bytes=64)
        slot_words = [keep.tile([P, SLOTS], U32, name=f"slot_words{a}", align_bytes=64) for a in range(PASSES)]
        slot_scales = keep.tile([P, SLOTS], U8, name="slot_scales", align_bytes=64)
        wq = keep.tile([P, E * PASSES * N], U32, name="wq", align_bytes=64)
        wq_scales = keep.tile([P, E * PASSES * N], U8, name="wq_scales", align_bytes=64)
        bias = keep.tile([P, E], F32, name="bias")
        gates = keep.tile([P, 2, T], F32, name="gates")
        y = keep.tile([P, SLOTS], F32, name="y")
        second = keep.tile([P, T], F32, name="second")
        part1 = keep.tile([P, T], F32, name="part1")
        part2 = keep.tile([P, T], F32, name="part2")
        total = keep.tile([P, T], F32, name="total")
        acc = [psum.tile([P, C], F32, name=f"acc{e}") for e in range(E)]

        def load_x(a, first, count):
            rows = xT[512 * a : 512 * (a + 1), :].rearrange("(p j) t -> p j t", j=4)
            nc.sync.dma_start(out=raw[a][:, first : first + count, :], in_=rows[:, first : first + count, :])

        load_x(0, 0, 2)
        load_x(0, 2, 2)
        nc.sync.dma_start(offs_sb[:], offs)
        load_x(1, 0, 2)
        load_x(1, 2, 2)
        load_x(2, 0, 4)

        nc.vector.memset(scales[:].bitcast(I32), 0)
        for a in range(LAST):
            nc.vector.memset(words[a][:, T:PITCH], 0)
        nc.gpsimd.memset(wq_scales[:].bitcast(I32), 0)

        for r in range(4):
            nc.sync.dma_start(
                out=wq_scales[r:P:32, :].bitcast(I32).rearrange("q (g n) -> q g n", g=E * PASSES),
                in_=w_scales[:, :, r:16:4, :].bitcast(I32).rearrange("e a q n -> q (e a) n"),
            )

        def load_weights(a, lo, hi):
            nc.sync.dma_start(
                out=wq[:].bitcast(I32).rearrange("p (e a n) -> p e a n", a=PASSES, n=N)[:, lo:hi, a, :],
                in_=w_words.rearrange("e a p n r -> p e a (n r)")[:, lo:hi, a, :].bitcast(I32),
            )

        for lo, hi in HALVES:
            for a in range(LAST):
                load_weights(a, lo, hi)
        nc.sync.dma_start(out=bias[:], in_=b)
        for lo, hi in HALVES:
            load_weights(LAST, lo, hi)
        nc.sync.dma_start(pos1_sb[:], pos1)
        nc.sync.dma_start(pos2_sb[:], pos2)
        for g in range(2):
            nc.sync.dma_start(out=gates[:, g, :], in_=gate[g])

        def round_pair(copy, a, first, lo, hi):
            copy(out=grouped[a][:, lo:hi, first : first + 2], in_=raw[a][:, first : first + 2, lo:hi].rearrange("p j t -> p t j"))

        def quantize(a, lo, hi):
            nc.vector.quantize_mx(
                out=words[a][:, lo:hi].bitcast(FP8X4),
                scales=scales[4 * a : P, lo:hi],
                in_=grouped[a][:, lo:hi, :].rearrange("p t j -> p (t j)"),
            )

        def quantize_pass(a):
            quantize(a, 0, HALF)
            quantize(a, HALF, T)

        def gather_words(a, lo, hi, width):
            nc.vector.tensor_copy(
                out=slot_words[a][:, lo:hi],
                in_=words[a][:, :width].bitcast(U32).indirect(offs_sb[:, lo // 16 : hi // 16]),
            )

        def multiply(a, e):
            slots = slice(e * C, (e + 1) * C)
            weight = slice((e * PASSES + a) * N, (e * PASSES + a + 1) * N)
            nc.tensor.matmul_mx(
                out=acc[e][:],
                lhsT=wq[:, weight].bitcast(FP8X4),
                lhsT_scale=wq_scales[:, weight],
                rhs=slot_words[a][:, slots].bitcast(FP8X4),
                rhs_scale=slot_scales[4 * a : P, slots],
                start=(a == 0),
                stop=(a == LAST),
            )

        def finish(lo, hi):
            gather_words(LAST, lo * C, hi * C, T)
            for e in range(lo, hi):
                multiply(LAST, e)
                cols = slice(e * C, (e + 1) * C)
                nc.scalar.activation(out=y[:, cols], in_=acc[e][:], func=IDENTITY, bias=bias[:, e : e + 1])

        round_pair(nc.vector.tensor_copy, 0, 0, 0, SCALAR_FROM)
        round_pair(nc.scalar.copy, 0, 0, SCALAR_FROM, T)
        round_pair(nc.vector.tensor_copy, 0, 2, 0, QUARTER)
        round_pair(nc.vector.tensor_copy, 0, 2, QUARTER, SCALAR_FROM)
        round_pair(nc.scalar.copy, 0, 2, 3 * QUARTER, T)
        round_pair(nc.scalar.copy, 0, 2, SCALAR_FROM, 3 * QUARTER)
        for quarter in (0, 3, 1, 2):
            quantize(0, quarter * QUARTER, (quarter + 1) * QUARTER)
        gather_words(0, 0, EARLY, PITCH)

        round_pair(nc.scalar.copy, 1, 0, GPSIMD_TO, T)
        round_pair(nc.scalar.copy, 1, 2, GPSIMD_TO, HALF)
        round_pair(nc.scalar.copy, 1, 2, HALF, T)
        for first in (0, 2):
            round_pair(nc.gpsimd.tensor_copy, 1, first, 0, GPSIMD_TO)
        quantize_pass(1)
        gather_words(0, EARLY, SLOTS, REACH)
        gather_words(1, 0, EARLY, PITCH)

        whole_in = raw[LAST][:].rearrange("p j t -> p t j")
        nc.gpsimd.tensor_copy(out=grouped[LAST][:, :GPSIMD_WHOLE, :], in_=whole_in[:, :GPSIMD_WHOLE, :])
        nc.scalar.copy(out=grouped[LAST][:, GPSIMD_WHOLE:HALF, :], in_=whole_in[:, GPSIMD_WHOLE:HALF, :])
        nc.scalar.copy(out=grouped[LAST][:, HALF:, :], in_=whole_in[:, HALF:, :])
        quantize_pass(LAST)
        gather_words(1, EARLY, SLOTS, REACH)

        for lo, hi in HALVES:
            nc.vector.tensor_copy(
                out=slot_scales[:, lo * C : hi * C],
                in_=scales[:].indirect(offs_sb[:, lo * C // 16 : hi * C // 16]),
            )
            for a in range(LAST):
                for e in range(lo, hi):
                    multiply(a, e)
        for lo, hi in LAST_GROUPS:
            finish(lo, hi)

        def second_product(lo, hi):
            nc.scalar.activation(out=second[:, lo:hi], in_=y[:].indirect(pos2_sb[:, lo // 16 : hi // 16]), func=COPY)
            nc.vector.tensor_tensor(out=part2[:, lo:hi], in0=second[:, lo:hi], in1=gates[:, 1, lo:hi], op=MULT)

        def add_and_store(lo, hi):
            nc.vector.tensor_tensor(out=total[:, lo:hi], in0=part1[:, lo:hi], in1=part2[:, lo:hi], op=ADD)
            nc.sync.dma_start(out=out[:, lo:hi], in_=total[:, lo:hi])

        nc.vector.tensor_tensor(out=part1[:], in0=y[:].indirect(pos1_sb[:]), in1=gates[:, 0, :], op=MULT)
        for lo, hi in ((0, HALF), (HALF, LAST_CUT), (LAST_CUT, T)):
            second_product(lo, hi)
        for lo, hi in ((0, FIRST_STORE), (FIRST_STORE, 3 * QUARTER), (3 * QUARTER, T)):
            add_and_store(lo, hi)
